import numpy as np
import ml_dtypes


def mxq(x, axis, fmt="e4m3"):
    dtype, down = {"e4m3": (ml_dtypes.float8_e4m3fn, 7), "e5m2": (ml_dtypes.float8_e5m2, 14)}[fmt]
    v = np.moveaxis(np.asarray(x, np.float32).astype(ml_dtypes.bfloat16).astype(np.float64), axis, -1)
    blocks = v.reshape(v.shape[:-1] + (-1, 32))
    amax = np.abs(blocks).max(-1, keepdims=True)
    byte = np.maximum(np.where(amax > 0, np.frexp(amax)[1] - 1 + 127, 0) - down, 1)
    scale = np.exp2(byte - 127.0)
    codes = (blocks / scale).astype(np.float32).astype(dtype).astype(np.float64)
    return np.moveaxis((codes * scale).reshape(v.shape), -1, axis)


WIDE = False


def mx_kscale(k):
    if not WIDE:
        return np.ones(k)
    levels = np.array([10, -10, 5, -5, 0])
    if k % 512:
        return np.exp2(np.random.permutation(np.resize(levels, k // 32))).repeat(32)
    a = np.empty((k // 512, 16))
    for p in range(k // 512):
        a[p, :8] = np.random.permutation(np.resize(levels, 8))
        for g in range(8):
            far = levels[np.abs(levels - a[p, g]) >= 10]
            a[p, g + 8] = far[np.random.randint(len(far))]
    return np.exp2(a.ravel()).repeat(32)


def f64(x):
    return np.asarray(x).astype(np.float64)


def striped(idx):
    return np.tile(idx.reshape(-1, 16).T, (8, 1)).astype(np.uint16)


def unstriped(offs):
    return offs[:16].T.reshape(-1).astype(np.int64)


def pack_weight(w):
    k, n = w.shape
    w = f64(np.asarray(w, np.float32).astype(ml_dtypes.bfloat16)).reshape(k // 32, 32, n)
    amax = np.abs(w).max(1)
    byte = np.clip(np.where(amax > 0, np.frexp(amax)[1] - 1 + 127 - 7, 1), 1, 254)
    scaled = (w * np.exp2(127.0 - byte)[:, None, :]).reshape(k, n).astype(np.float32)
    words = np.ascontiguousarray(scaled.reshape(k // 512, 128, 4, n).transpose(0, 1, 3, 2)).astype(ml_dtypes.float8_e4m3fn).view(np.uint8)
    return words, np.ascontiguousarray(byte.astype(np.uint8).reshape(k // 512, 16, n))


def unpack_weight(words, scales):
    g, p, n, _ = words.shape
    vals = np.ascontiguousarray(words).view(ml_dtypes.float8_e4m3fn).astype(np.float64) * np.repeat(np.exp2(scales.astype(np.float64) - 127.0), 8, axis=1)[..., None]
    return vals.transpose(0, 1, 3, 2).reshape(g * 512, n)

def planes(y):
    n, m = y.shape
    v = y.astype(np.float32).astype(ml_dtypes.bfloat16).astype(np.float64).reshape(n // 32, 32, m)
    top = np.abs(v).max(1)
    byte = np.clip(np.where(top > 0, np.frexp(top)[1] - 1 + 127 - 7, 1), 1, 254)
    codes = (v * np.exp2(127.0 - byte)[:, None, :]).reshape(n, m).astype(np.float32).astype(ml_dtypes.float8_e4m3fn).view(np.uint8)
    words = codes.reshape(n // 512, 128, 4, m).transpose(0, 1, 3, 2)
    return np.ascontiguousarray(words), np.ascontiguousarray(byte.astype(np.uint8).reshape(n // 512, 16, m))


K, T, S, V, N, U = 512, 1024, 512, 256, 512, 512


def setup_inputs():
    n = np.random.standard_normal
    s = mx_kscale(K)[:, None]
    packed_xT = pack_weight(n((K, T)) * s)
    return {
        "x_words": packed_xT[0],
        "x_scales": packed_xT[1],
        "w1": (n((K, N)) / np.sqrt(2 * K) / s).astype(np.float32),
        "w2": (n((K, N)) / np.sqrt(2 * K) / s).astype(np.float32),
        "offs": striped(np.random.permutation(T)[:S]),
        "to1": striped(np.random.permutation(U)[:V]),
        "to2": striped(np.random.permutation(U)[:V]),
    }


def reference(x_words, x_scales, w1, w2, offs, to1, to2):
    xq = unpack_weight(x_words, x_scales)[:, unstriped(offs)]
    o0 = np.zeros((N, S))
    o0[:, unstriped(to1)] = mxq(f64(w1), 0, "e4m3").T @ xq[:, :V]
    o1 = np.zeros((N, S))
    o1[:, unstriped(to2)] = mxq(f64(w2), 0, "e4m3").T @ xq[:, V:2 * V]
    out_0 = o0 + o1
    return (out_0,) + planes(out_0)

@@ -1,0 +1,148 @@
+from contextlib import ExitStack
+
+import concourse.mybir as mybir
+
+K, T, S, V, N, U = 512, 1024, 512, 256, 512, 512
+FLOPS = 2 * 2 * K * N * V
+
+F32 = mybir.dt.float32
+BF16 = mybir.dt.bfloat16
+I32 = mybir.dt.int32
+U32 = mybir.dt.uint32
+U16 = mybir.dt.uint16
+U8 = mybir.dt.uint8
+FP8X4 = mybir.dt.float8_e4m3fn_x4
+ADD = mybir.AluOpType.add
+COPY = mybir.ActivationFunctionType.Copy
+
+P = 128
+PACK = 4
+HALF = N // 2
+
+
+def tile_picked_spconv_none_po_kernel(
+    tc, x_words, x_scales, w1, w2, offs, to1, to2, out_0, out_1, out_2
+):
+    nc = tc.nc
+    with ExitStack() as ctx:
+        sb = ctx.enter_context(tc.tile_pool(name="sb", bufs=1))
+        ps = ctx.enter_context(tc.psum_pool(name="ps", bufs=1))
+
+        offs_t = sb.tile([P, S // 16], U16, name="offs_t")
+        to_t = [sb.tile([P, V // 16], U16, name=f"to_t{d}") for d in range(2)]
+        xw = sb.tile([P, T], I32, name="xw", align_bytes=64)
+        xs = sb.tile([P, T], U8, name="xs", align_bytes=64)
+        raw = [[sb.tile([P, PACK, HALF], F32, name=f"raw{d}{h}", tag=f"raw{d}{h}") for h in range(2)] for d in range(2)]
+        wb = [sb.tile([P, PACK, P, PACK], BF16, name=f"wb{d}", align_bytes=64) for d in range(2)]
+        wc = [sb.tile([P, N], U32, name=f"wc{d}", align_bytes=64) for d in range(2)]
+        ws = [sb.tile([P, N], U8, name=f"ws{d}", align_bytes=64) for d in range(2)]
+        gw = [sb.tile([P, V], U32, name=f"gw{d}", align_bytes=64) for d in range(2)]
+        gs = sb.tile([P, S], U8, name="gs", align_bytes=64)
+        win = [[sb.tile([P, U], F32, name=f"win{d}{t}") for t in range(PACK)] for d in range(2)]
+        total = sb.tile([P, PACK, U], F32, name="total")
+        ob = sb.tile([P, U, PACK], BF16, name="ob", align_bytes=64)
+        oc = sb.tile([P, U], I32, name="oc", align_bytes=64)
+        osc = sb.tile([P, U], U8, name="osc", align_bytes=64)
+
+        w_rows = [w.rearrange("(p j) m -> p j m", j=PACK) for w in (w1, w2)]
+
+        nc.gpsimd.memset(xs[:].bitcast(I32), 0)
+        nc.sync.dma_start(raw[0][0][:], w_rows[0][:, :, 0:HALF])
+        nc.sync.dma_start(offs_t[:], offs)
+        for q in range(4):
+            nc.sync.dma_start(
+                xs[32 * q : 32 * q + 4, :].bitcast(I32), x_scales[0, 4 * q : 4 * q + 4, :].bitcast(I32)
+            )
+        nc.sync.dma_start(raw[0][1][:], w_rows[0][:, :, HALF:N])
+        nc.sync.dma_start(xw[:], x_words[0].rearrange("p n r -> p (n r)").bitcast(I32))
+        nc.sync.dma_start(to_t[0][:], to1)
+        for h in range(2):
+            nc.sync.dma_start(raw[1][h][:], w_rows[1][:, :, h * HALF : (h + 1) * HALF])
+        nc.sync.dma_start(to_t[1][:], to2)
+
+        for d in range(2):
+            for t in range(PACK):
+                nc.vector.memset(win[d][t][:], 0.0)
+
+        def deal(eng, d, h, a, b):
+            src = raw[d][h][:].rearrange("p j (m t) -> p m j t", t=PACK)[:, a:b]
+            dst = wb[d][:].rearrange("p t m j -> p m j t")[:, 64 * h + a : 64 * h + b]
+            eng(dst, src)
+
+        def quant_w(d, t0, t1):
+            nc.vector.quantize_mx(
+                out=wc[d][:, t0 * P : t1 * P].bitcast(FP8X4),
+                scales=ws[d][:, t0 * P : t1 * P],
+                in_=wb[d][:, t0:t1].rearrange("p t m j -> p (t m j)"),
+            )
+
+        nc.vector.tensor_copy(gs[:], xs[:].indirect(offs_t[:]))
+        deal(nc.scalar.copy, 0, 0, 0, 64)
+        deal(nc.scalar.copy, 0, 1, 0, 20)
+        deal(nc.vector.tensor_copy, 0, 1, 20, 64)
+        quant_w(0, 0, 4)
+        for d in range(2):
+            nc.vector.tensor_copy(gw[d][:], xw[:].bitcast(U32).indirect(offs_t[:, 16 * d : 16 * d + 16]))
+
+        ys = {}
+        tags = {(0, 3): "raw11"}
+
+        def product(d, t):
+            acc = ps.tile([P, V], F32, name=f"acc{d}{t}")
+            nc.tensor.matmul_mx(
+                out=acc[:],
+                lhsT=wc[d][:, t * P : (t + 1) * P].bitcast(FP8X4),
+                lhsT_scale=ws[d][:, t * P : (t + 1) * P],
+                rhs=gw[d][:].bitcast(FP8X4),
+                rhs_scale=gs[:, d * V : (d + 1) * V],
+                start=True,
+                stop=True,
+            )
+            ys[d, t] = sb.tile([P, V], F32, name=f"y{d}{t}", tag=tags.get((d, t), f"y{d}{t}"))
+            nc.scalar.copy(ys[d, t][:], acc[:])
+
+        def scatter(d, t):
+            nc.vector.tensor_copy(win[d][t][:].indirect(to_t[d][:]), ys[d, t][:])
+
+        out_rows = out_0.rearrange("(p t) u -> p t u", t=PACK)
+
+        def add(t, a, b):
+            eng = nc.vector if t < 3 else nc.vector
+            eng.tensor_tensor(total[:, t, a:b], win[0][t][:, a:b], win[1][t][:, a:b], ADD)
+
+        def weave(eng, t0, a, b):
+            eng(ob[:, a:b, t0 : t0 + 2], total[:, t0 : t0 + 2, a:b].rearrange("p t u -> p u t"))
+
+        for t in range(3):
+            product(0, t)
+        for h in range(2):
+            deal(nc.scalar.copy, 1, h, 0, 64)
+        product(0, 3)
+        for t in range(3):
+            scatter(0, t)
+        quant_w(1, 0, 4)
+        for t in range(PACK):
+            product(1, t)
+        scatter(0, 3)
+        for t in range(PACK - 1):
+            scatter(1, t)
+            add(t, 0, U)
+            nc.sync.dma_start(out_rows[:, t, :], total[:, t, :])
+            if t == 1:
+                weave(nc.scalar.copy, 0, 0, U)
+        scatter(1, 3)
+        words = out_1[0].rearrange("p u r -> p (u r)").bitcast(I32)
+        for h in range(2):
+            add(3, h * 256, (h + 1) * 256)
+        nc.sync.dma_start(out_rows[:, 3, :], total[:, 3, :])
+        for h in range(2):
+            weave(nc.vector.tensor_copy, 2, h * 256, (h + 1) * 256)
+        for h in range(2):
+            c = slice(h * 256, (h + 1) * 256)
+            nc.vector.quantize_mx(
+                out=oc[:, c].bitcast(FP8X4), scales=osc[:, c], in_=ob[:, c, :].rearrange("p u t -> p (u t)")
+            )
+            nc.sync.dma_start(words[:, c], oc[:, c])
+        for q in range(4):
+            eng = nc.scalar if q % 2 else nc.sync
+            eng.dma_start(out_2[0, 4 * q : 4 * q + 4, :].bitcast(I32), osc[32 * q : 32 * q + 4, :].bitcast(I32))

@@ -38,7 +38,8 @@ def tile_picked_spconv_none_po_kernel(
         ws = [sb.tile([P, N], U8, name=f"ws{d}", align_bytes=64) for d in range(2)]
         gw = [sb.tile([P, V], U32, name=f"gw{d}", align_bytes=64) for d in range(2)]
         gs = sb.tile([P, S], U8, name="gs", align_bytes=64)
-        win = [[sb.tile([P, U], F32, name=f"win{d}{t}") for t in range(PACK)] for d in range(2)]
+        wins = [[sb.tile([P, U], F32, name=f"win{d}{i}") for i in range(3 - d)] for d in range(2)]
+        win = [[wins[d][t % (3 - d)] for t in range(PACK)] for d in range(2)]
         total = sb.tile([P, PACK, U], F32, name="total")
         ob = sb.tile([P, U, PACK], BF16, name="ob", align_bytes=64)
         oc = sb.tile([P, U], I32, name="oc", align_bytes=64)
@@ -61,8 +62,8 @@ def tile_picked_spconv_none_po_kernel(
         nc.sync.dma_start(to_t[1][:], to2)
 
         for d in range(2):
-            for t in range(PACK):
-                nc.vector.memset(win[d][t][:], 0.0)
+            for w in wins[d]:
+                nc.vector.memset(w[:], 0.0)
 
         def deal(eng, d, h, a, b):
             src = raw[d][h][:].rearrange("p j (m t) -> p m j t", t=PACK)[:, a:b]
@@ -81,62 +82,72 @@ def tile_picked_spconv_none_po_kernel(
         deal(nc.scalar.copy, 0, 1, 0, 20)
         deal(nc.vector.tensor_copy, 0, 1, 20, 64)
         quant_w(0, 0, 4)
-        for d in range(2):
-            nc.vector.tensor_copy(gw[d][:], xw[:].bitcast(U32).indirect(offs_t[:, 16 * d : 16 * d + 16]))
+        for d, a, b in ((0, 0, 128), (0, 128, 256), (1, 0, 256)):
+            nc.vector.tensor_copy(
+                gw[d][:, a:b], xw[:].bitcast(U32).indirect(offs_t[:, 16 * d + a // 16 : 16 * d + b // 16])
+            )
 
         ys = {}
-        tags = {(0, 3): "raw11"}
+        tags = {(0, 2): "raw11"}
 
-        def product(d, t):
-            acc = ps.tile([P, V], F32, name=f"acc{d}{t}")
+        def product(d, t, a=0, b=V):
+            acc = ps.tile([P, b - a], F32, name=f"acc{d}{t}{a}", tag=f"acc{t}{d if a == 0 else 1}")
             nc.tensor.matmul_mx(
                 out=acc[:],
                 lhsT=wc[d][:, t * P : (t + 1) * P].bitcast(FP8X4),
                 lhsT_scale=ws[d][:, t * P : (t + 1) * P],
-                rhs=gw[d][:].bitcast(FP8X4),
-                rhs_scale=gs[:, d * V : (d + 1) * V],
+                rhs=gw[d][:, a:b].bitcast(FP8X4),
+                rhs_scale=gs[:, d * V + a : d * V + b],
                 start=True,
                 stop=True,
             )
-            ys[d, t] = sb.tile([P, V], F32, name=f"y{d}{t}", tag=tags.get((d, t), f"y{d}{t}"))
-            nc.scalar.copy(ys[d, t][:], acc[:])
+            ys[d, t, a] = sb.tile([P, b - a], F32, name=f"y{d}{t}{a}", tag=tags.get((d, t), f"y{d}{t}{a}"))
+            nc.scalar.copy(ys[d, t, a][:], acc[:])
 
-        def scatter(d, t):
-            nc.vector.tensor_copy(win[d][t][:].indirect(to_t[d][:]), ys[d, t][:])
+        def scatter(d, t, a=0, b=V):
+            nc.vector.tensor_copy(win[d][t][:].indirect(to_t[d][:, a // 16 : b // 16]), ys[d, t, a][:])
 
         out_rows = out_0.rearrange("(p t) u -> p t u", t=PACK)
 
         def add(t, a, b):
-            eng = nc.vector if t < 3 else nc.vector
+            eng = nc.gpsimd if t < 3 else nc.vector
             eng.tensor_tensor(total[:, t, a:b], win[0][t][:, a:b], win[1][t][:, a:b], ADD)
 
         def weave(eng, t0, a, b):
             eng(ob[:, a:b, t0 : t0 + 2], total[:, t0 : t0 + 2, a:b].rearrange("p t u -> p u t"))
 
-        for t in range(3):
-            product(0, t)
+        product(0, 0, 0, 128)
+        product(0, 1)
+        product(0, 0, 128, 256)
         for h in range(2):
             deal(nc.scalar.copy, 1, h, 0, 64)
-        product(0, 3)
-        for t in range(3):
-            scatter(0, t)
+        product(0, 2)
+        scatter(0, 0, 0, 128)
+        scatter(0, 1)
+        scatter(0, 0, 128, 256)
         quant_w(1, 0, 4)
+        scatter(0, 2)
         for t in range(PACK):
             product(1, t)
-        scatter(0, 3)
+        product(0, 3)
         for t in range(PACK - 1):
             scatter(1, t)
             add(t, 0, U)
             nc.sync.dma_start(out_rows[:, t, :], total[:, t, :])
             if t == 1:
                 weave(nc.scalar.copy, 0, 0, U)
+        scatter(0, 3)
         scatter(1, 3)
         words = out_1[0].rearrange("p u r -> p (u r)").bitcast(I32)
-        for h in range(2):
-            add(3, h * 256, (h + 1) * 256)
+        cut = 192
+        mid = (cut + U) // 2
+        add(3, 0, cut)
+        weave(nc.scalar.copy, 2, 0, cut)
+        add(3, cut, mid)
+        add(3, mid, U)
         nc.sync.dma_start(out_rows[:, 3, :], total[:, 3, :])
-        for h in range(2):
-            weave(nc.vector.tensor_copy, 2, h * 256, (h + 1) * 256)
+        weave(nc.vector.tensor_copy, 2, cut, mid)
+        weave(nc.vector.tensor_copy, 2, mid, U)
         for h in range(2):
             c = slice(h * 256, (h + 1) * 256)
             nc.vector.quantize_mx(

@@ -32,14 +32,20 @@ def tile_picked_spconv_none_po_kernel(
         to_t = [sb.tile([P, V // 16], U16, name=f"to_t{d}") for d in range(2)]
         xw = sb.tile([P, T], I32, name="xw", align_bytes=64)
         xs = sb.tile([P, T], U8, name="xs", align_bytes=64)
-        raw = [[sb.tile([P, PACK, HALF], F32, name=f"raw{d}{h}", tag=f"raw{d}{h}") for h in range(2)] for d in range(2)]
-        wb = [sb.tile([P, PACK, P, PACK], BF16, name=f"wb{d}", align_bytes=64) for d in range(2)]
-        wc = [sb.tile([P, N], U32, name=f"wc{d}", align_bytes=64) for d in range(2)]
+        raw = [sb.tile([P, PACK, HALF], F32, name=f"raw{h}", tag=f"raw{h}") for h in range(2)]
+        raw2 = [sb.tile([P, PACK, HALF], F32, name=f"raw2{h}", tag=f"raw2{h}") for h in range(2)]
+        wc_a = sb.tile([P, 2 * P], U32, name="wc_a", tag="mid0", align_bytes=64)
+        wc_rest = sb.tile([P, 2 * P], U32, name="wc_rest", align_bytes=64)
+        wc2 = sb.tile([P, N], U32, name="wc2", align_bytes=64)
+        codes = [
+            [wc_a[:, 0:P], wc_a[:, P : 2 * P], wc_rest[:, 0:P], wc_rest[:, P : 2 * P]],
+            [wc2[:, t * P : (t + 1) * P] for t in range(PACK)],
+        ]
         ws = [sb.tile([P, N], U8, name=f"ws{d}", align_bytes=64) for d in range(2)]
-        gw = [sb.tile([P, V], U32, name=f"gw{d}", align_bytes=64) for d in range(2)]
         gs = sb.tile([P, S], U8, name="gs", align_bytes=64)
-        wins = [[sb.tile([P, U], F32, name=f"win{d}{i}") for i in range(3 - d)] for d in range(2)]
-        win = [[wins[d][t % (3 - d)] for t in range(PACK)] for d in range(2)]
+        wins = [[sb.tile([P, U], F32, name=f"win{d}{i}") for i in range(4 - d)] for d in range(2)]
+        win = [[wins[d][t % (4 - d)] for t in range(PACK)] for d in range(2)]
+        first = [sb.tile([P, U], F32, name=f"first{t}") for t in range(PACK)]
         total = sb.tile([P, PACK, U], F32, name="total")
         ob = sb.tile([P, U, PACK], BF16, name="ob", align_bytes=64)
         oc = sb.tile([P, U], I32, name="oc", align_bytes=64)
@@ -47,96 +53,122 @@ def tile_picked_spconv_none_po_kernel(
 
         w_rows = [w.rearrange("(p j) m -> p j m", j=PACK) for w in (w1, w2)]
 
-        nc.gpsimd.memset(xs[:].bitcast(I32), 0)
-        nc.sync.dma_start(raw[0][0][:], w_rows[0][:, :, 0:HALF])
         nc.sync.dma_start(offs_t[:], offs)
         for q in range(4):
-            nc.sync.dma_start(
-                xs[32 * q : 32 * q + 4, :].bitcast(I32), x_scales[0, 4 * q : 4 * q + 4, :].bitcast(I32)
-            )
-        nc.sync.dma_start(raw[0][1][:], w_rows[0][:, :, HALF:N])
+            rows = x_scales[0, 4 * q : 4 * q + 4, :].bitcast(I32)
+            nc.sync.dma_start(xs[32 * q : 32 * q + 32, :].bitcast(I32), rows.partition_broadcast(8))
+        nc.sync.dma_start(raw[0][:], w_rows[0][:, :, 0:HALF])
         nc.sync.dma_start(xw[:], x_words[0].rearrange("p n r -> p (n r)").bitcast(I32))
         nc.sync.dma_start(to_t[0][:], to1)
+        nc.sync.dma_start(raw[1][:], w_rows[0][:, :, HALF:N])
         for h in range(2):
-            nc.sync.dma_start(raw[1][h][:], w_rows[1][:, :, h * HALF : (h + 1) * HALF])
+            nc.sync.dma_start(raw2[h][:], w_rows[1][:, :, h * HALF : (h + 1) * HALF])
         nc.sync.dma_start(to_t[1][:], to2)
 
         for d in range(2):
             for w in wins[d]:
-                nc.vector.memset(w[:], 0.0)
+                (nc.gpsimd if d else nc.vector).memset(w[:], 0.0)
 
-        def deal(eng, d, h, a, b):
-            src = raw[d][h][:].rearrange("p j (m t) -> p m j t", t=PACK)[:, a:b]
-            dst = wb[d][:].rearrange("p t m j -> p m j t")[:, 64 * h + a : 64 * h + b]
+        def deal_first(eng, h, rounded, a, b):
+            src = raw[h][:].rearrange("p j (l t) -> p l j t", t=PACK)[:, a:b]
+            dst = rounded[:].rearrange("p t l j -> p l j t")[:, a:b]
             eng(dst, src)
 
-        def quant_w(d, t0, t1):
+        def deal_second(h):
+            src = raw2[h][:].rearrange("p j (m t) -> p m j t", t=PACK)
+            dst = wb2[:].rearrange("p t m j -> p m j t")[:, 64 * h : 64 * h + 64]
+            nc.scalar.copy(dst, src)
+
+        def quant_w(d, t0, t1, words, rounded):
             nc.vector.quantize_mx(
-                out=wc[d][:, t0 * P : t1 * P].bitcast(FP8X4),
+                out=words.bitcast(FP8X4),
                 scales=ws[d][:, t0 * P : t1 * P],
-                in_=wb[d][:, t0:t1].rearrange("p t m j -> p (t m j)"),
+                in_=rounded,
             )
 
-        nc.vector.tensor_copy(gs[:], xs[:].indirect(offs_t[:]))
-        deal(nc.scalar.copy, 0, 0, 0, 64)
-        deal(nc.scalar.copy, 0, 1, 0, 20)
-        deal(nc.vector.tensor_copy, 0, 1, 20, 64)
-        quant_w(0, 0, 4)
-        for d, a, b in ((0, 0, 128), (0, 128, 256), (1, 0, 256)):
-            nc.vector.tensor_copy(
-                gw[d][:, a:b], xw[:].bitcast(U32).indirect(offs_t[:, 16 * d + a // 16 : 16 * d + b // 16])
-            )
+        def gather_words(a, b):
+            nc.vector.tensor_copy(gw[:, a:b], xw[:].bitcast(U32).indirect(offs_t[:, a // 16 : b // 16]))
 
         ys = {}
-        tags = {(0, 2): "raw11"}
+        tags = {(0, 1): "raw1", (0, 3): "raw21"}
 
-        def product(d, t, a=0, b=V):
-            acc = ps.tile([P, b - a], F32, name=f"acc{d}{t}{a}", tag=f"acc{t}{d if a == 0 else 1}")
+        def multiply(d, t, a, b, acc):
             nc.tensor.matmul_mx(
                 out=acc[:],
-                lhsT=wc[d][:, t * P : (t + 1) * P].bitcast(FP8X4),
+                lhsT=codes[d][t].bitcast(FP8X4),
                 lhsT_scale=ws[d][:, t * P : (t + 1) * P],
-                rhs=gw[d][:, a:b].bitcast(FP8X4),
+                rhs=gw[:, d * V + a : d * V + b].bitcast(FP8X4),
                 rhs_scale=gs[:, d * V + a : d * V + b],
                 start=True,
                 stop=True,
             )
+
+        def empty(d, t, a, b, acc):
             ys[d, t, a] = sb.tile([P, b - a], F32, name=f"y{d}{t}{a}", tag=tags.get((d, t), f"y{d}{t}{a}"))
             nc.scalar.copy(ys[d, t, a][:], acc[:])
 
+        def product(d, t, a=0, b=V):
+            acc = ps.tile([P, b - a], F32, name=f"acc{d}{t}{a}", tag=f"acc{len(ys) % 8}")
+            multiply(d, t, a, b, acc)
+            empty(d, t, a, b, acc)
+
         def scatter(d, t, a=0, b=V):
             nc.vector.tensor_copy(win[d][t][:].indirect(to_t[d][:, a // 16 : b // 16]), ys[d, t, a][:])
+
+        def move(blk):
+            h, pair = divmod(blk, 2)
+            for e in range(2):
+                nc.sync.dma_start(first[2 * pair + e][64 * h : 64 * h + 64, :], win[0][blk][64 * e : 64 * e + 64, :])
 
         out_rows = out_0.rearrange("(p t) u -> p t u", t=PACK)
 
         def add(t, a, b):
             eng = nc.gpsimd if t < 3 else nc.vector
-            eng.tensor_tensor(total[:, t, a:b], win[0][t][:, a:b], win[1][t][:, a:b], ADD)
+            eng.tensor_tensor(total[:, t, a:b], first[t][:, a:b], win[1][t][:, a:b], ADD)
 
         def weave(eng, t0, a, b):
             eng(ob[:, a:b, t0 : t0 + 2], total[:, t0 : t0 + 2, a:b].rearrange("p t u -> p u t"))
 
+        nc.vector.tensor_copy(gs[:], xs[:].indirect(offs_t[:]))
+        wb_a = sb.tile([P, PACK, 64, PACK], BF16, name="wb_a", tag="early0", align_bytes=64)
+        deal_first(nc.vector.tensor_copy, 0, wb_a, 0, 40)
+        deal_first(nc.scalar.copy, 0, wb_a, 40, 64)
+        quant_w(0, 0, 2, wc_a[:], wb_a[:].rearrange("p t m j -> p (t m j)"))
+        gw = sb.tile([P, S], U32, name="gw", tag="early0", align_bytes=64)
+        gather_words(0, 128)
+        gather_words(128, V)
+        gather_words(V, S)
         product(0, 0, 0, 128)
-        product(0, 1)
         product(0, 0, 128, 256)
-        for h in range(2):
-            deal(nc.scalar.copy, 1, h, 0, 64)
-        product(0, 2)
+        held = ps.tile([P, V], F32, name="held", tag="acc2")
+        multiply(0, 1, 0, V, held)
+        wb_rest = sb.tile([P, PACK, 64, PACK], BF16, name="wb_rest", tag="mid0", align_bytes=64)
+        deal_first(nc.scalar.copy, 1, wb_rest, 0, 64)
+        empty(0, 1, 0, V, held)
         scatter(0, 0, 0, 128)
-        scatter(0, 1)
         scatter(0, 0, 128, 256)
-        quant_w(1, 0, 4)
+        move(0)
+        quant_w(0, 2, 4, wc_rest[:], wb_rest[:].rearrange("p t m j -> p (t m j)"))
+        scatter(0, 1)
+        move(1)
+        wb2 = sb.tile([P, PACK, P, PACK], BF16, name="wb2", tag="mid0", align_bytes=64)
+        deal_second(0)
+        product(0, 2)
+        deal_second(1)
+        product(0, 3)
         scatter(0, 2)
+        move(2)
+        quant_w(1, 0, 4, wc2[:], wb2[:].rearrange("p t m j -> p (t m j)"))
+        scatter(0, 3)
+        move(3)
         for t in range(PACK):
             product(1, t)
-        product(0, 3)
         for t in range(PACK - 1):
             scatter(1, t)
             add(t, 0, U)
             nc.sync.dma_start(out_rows[:, t, :], total[:, t, :])
             if t == 1:
                 weave(nc.scalar.copy, 0, 0, U)
-        scatter(0, 3)
         scatter(1, 3)
         words = out_1[0].rearrange("p u r -> p (u r)").bitcast(I32)
         cut = 192

@@ -13,6 +13,7 @@ U16 = mybir.dt.uint16
 U8 = mybir.dt.uint8
 FP8X4 = mybir.dt.float8_e4m3fn_x4
 ADD = mybir.AluOpType.add
+MULT = mybir.AluOpType.mult
 COPY = mybir.ActivationFunctionType.Copy
 
 P = 128
@@ -32,7 +33,7 @@ def tile_picked_spconv_none_po_kernel(
         to_t = [sb.tile([P, V // 16], U16, name=f"to_t{d}") for d in range(2)]
         xw = sb.tile([P, T], I32, name="xw", align_bytes=64)
         xs = sb.tile([P, T], U8, name="xs", align_bytes=64)
-        raw = [sb.tile([P, PACK, HALF], F32, name=f"raw{h}", tag=f"raw{h}") for h in range(2)]
+        raw = [sb.tile([P, PACK, HALF], F32, name=f"raw{h}", tag=f"raw{h}", align_bytes=64) for h in range(2)]
         raw2 = [sb.tile([P, PACK, HALF], F32, name=f"raw2{h}", tag=f"raw2{h}") for h in range(2)]
         wc_a = sb.tile([P, 2 * P], U32, name="wc_a", tag="mid0", align_bytes=64)
         wc_rest = sb.tile([P, 2 * P], U32, name="wc_rest", align_bytes=64)
@@ -74,10 +75,14 @@ def tile_picked_spconv_none_po_kernel(
             dst = rounded[:].rearrange("p t l j -> p l j t")[:, a:b]
             eng(dst, src)
 
-        def deal_second(h):
-            src = raw2[h][:].rearrange("p j (m t) -> p m j t", t=PACK)
-            dst = wb2[:].rearrange("p t m j -> p m j t")[:, 64 * h : 64 * h + 64]
-            nc.scalar.copy(dst, src)
+        def pool_copy(dst, src):
+            order = "p m j t -> p m t j"
+            nc.gpsimd.tensor_scalar(dst.rearrange(order), src.rearrange(order), 1.0, 0.0, MULT, ADD)
+
+        def deal_second(eng, h, a, b):
+            src = raw2[h][:].rearrange("p j (m t) -> p m j t", t=PACK)[:, a:b]
+            dst = wb2[:].rearrange("p t m j -> p m j t")[:, 64 * h + a : 64 * h + b]
+            eng(dst, src)
 
         def quant_w(d, t0, t1, words, rounded):
             nc.vector.quantize_mx(
@@ -90,11 +95,11 @@ def tile_picked_spconv_none_po_kernel(
             nc.vector.tensor_copy(gw[:, a:b], xw[:].bitcast(U32).indirect(offs_t[:, a // 16 : b // 16]))
 
         ys = {}
-        tags = {(0, 1): "raw1", (0, 3): "raw21"}
+        tags = {(0, 3): "raw21"}
 
         def multiply(d, t, a, b, acc):
             nc.tensor.matmul_mx(
-                out=acc[:],
+                out=acc,
                 lhsT=codes[d][t].bitcast(FP8X4),
                 lhsT_scale=ws[d][:, t * P : (t + 1) * P],
                 rhs=gw[:, d * V + a : d * V + b].bitcast(FP8X4),
@@ -106,14 +111,15 @@ def tile_picked_spconv_none_po_kernel(
         def empty(d, t, a, b, acc):
             ys[d, t, a] = sb.tile([P, b - a], F32, name=f"y{d}{t}{a}", tag=tags.get((d, t), f"y{d}{t}{a}"))
             nc.scalar.copy(ys[d, t, a][:], acc[:])
+            ys[d, t, a] = ys[d, t, a][:]
 
         def product(d, t, a=0, b=V):
             acc = ps.tile([P, b - a], F32, name=f"acc{d}{t}{a}", tag=f"acc{len(ys) % 8}")
-            multiply(d, t, a, b, acc)
+            multiply(d, t, a, b, acc[:])
             empty(d, t, a, b, acc)
 
         def scatter(d, t, a=0, b=V):
-            nc.vector.tensor_copy(win[d][t][:].indirect(to_t[d][:, a // 16 : b // 16]), ys[d, t, a][:])
+            nc.vector.tensor_copy(win[d][t][:].indirect(to_t[d][:, a // 16 : b // 16]), ys[d, t, a])
 
         def move(blk):
             h, pair = divmod(blk, 2)
@@ -130,31 +136,36 @@ def tile_picked_spconv_none_po_kernel(
             eng(ob[:, a:b, t0 : t0 + 2], total[:, t0 : t0 + 2, a:b].rearrange("p t u -> p u t"))
 
         nc.vector.tensor_copy(gs[:], xs[:].indirect(offs_t[:]))
-        wb_a = sb.tile([P, PACK, 64, PACK], BF16, name="wb_a", tag="early0", align_bytes=64)
-        deal_first(nc.vector.tensor_copy, 0, wb_a, 0, 40)
-        deal_first(nc.scalar.copy, 0, wb_a, 40, 64)
+        wb_a = sb.tile([P, PACK, 64, PACK], BF16, name="wb_a", align_bytes=64)
+        deal_first(nc.vector.tensor_copy, 0, wb_a, 0, 38)
+        deal_first(nc.scalar.copy, 0, wb_a, 38, 64)
         quant_w(0, 0, 2, wc_a[:], wb_a[:].rearrange("p t m j -> p (t m j)"))
-        gw = sb.tile([P, S], U32, name="gw", tag="early0", align_bytes=64)
+        gw = sb.tile([P, S], U32, name="gw", tag="raw0", align_bytes=64)
         gather_words(0, 128)
         gather_words(128, V)
         gather_words(V, S)
         product(0, 0, 0, 128)
-        product(0, 0, 128, 256)
-        held = ps.tile([P, V], F32, name="held", tag="acc2")
-        multiply(0, 1, 0, V, held)
+        product(0, 1, 0, 128)
+        held = ps.tile([P, 2, 128], F32, name="held", tag="acc2")
+        for blk in range(2):
+            multiply(0, blk, 128, V, held[:, blk])
         wb_rest = sb.tile([P, PACK, 64, PACK], BF16, name="wb_rest", tag="mid0", align_bytes=64)
-        deal_first(nc.scalar.copy, 1, wb_rest, 0, 64)
-        empty(0, 1, 0, V, held)
-        scatter(0, 0, 0, 128)
-        scatter(0, 0, 128, 256)
-        move(0)
+        deal_first(pool_copy, 1, wb_rest, 0, 20)
+        deal_first(nc.scalar.copy, 1, wb_rest, 20, 64)
+        y_held = sb.tile([P, 2, 128], F32, name="y_held", tag="raw1", align_bytes=64)
+        nc.scalar.copy(y_held[:], held[:])
+        for blk in range(2):
+            ys[0, blk, 128] = y_held[:, blk]
+            scatter(0, blk, 0, 128)
         quant_w(0, 2, 4, wc_rest[:], wb_rest[:].rearrange("p t m j -> p (t m j)"))
-        scatter(0, 1)
-        move(1)
+        for blk in range(2):
+            scatter(0, blk, 128, V)
+            move(blk)
         wb2 = sb.tile([P, PACK, P, PACK], BF16, name="wb2", tag="mid0", align_bytes=64)
-        deal_second(0)
+        deal_second(pool_copy, 0, 0, 40)
+        deal_second(nc.scalar.copy, 0, 40, 64)
         product(0, 2)
-        deal_second(1)
+        deal_second(nc.scalar.copy, 1, 0, 64)
         product(0, 3)
         scatter(0, 2)
         move(2)

@@ -33,20 +33,12 @@ def tile_picked_spconv_none_po_kernel(
         to_t = [sb.tile([P, V // 16], U16, name=f"to_t{d}") for d in range(2)]
         xw = sb.tile([P, T], I32, name="xw", align_bytes=64)
         xs = sb.tile([P, T], U8, name="xs", align_bytes=64)
-        raw = [sb.tile([P, PACK, HALF], F32, name=f"raw{h}", tag=f"raw{h}", align_bytes=64) for h in range(2)]
-        raw2 = [sb.tile([P, PACK, HALF], F32, name=f"raw2{h}", tag=f"raw2{h}") for h in range(2)]
-        wc_a = sb.tile([P, 2 * P], U32, name="wc_a", tag="mid0", align_bytes=64)
-        wc_rest = sb.tile([P, 2 * P], U32, name="wc_rest", align_bytes=64)
-        wc2 = sb.tile([P, N], U32, name="wc2", align_bytes=64)
-        codes = [
-            [wc_a[:, 0:P], wc_a[:, P : 2 * P], wc_rest[:, 0:P], wc_rest[:, P : 2 * P]],
-            [wc2[:, t * P : (t + 1) * P] for t in range(PACK)],
-        ]
+        raw = [[sb.tile([P, PACK, HALF], F32, name=f"raw{d}{h}", tag=f"raw{d}{h}", align_bytes=64) for h in range(2)] for d in range(2)]
+        wb = [sb.tile([P, PACK, P, PACK], BF16, name=f"wb{d}", align_bytes=64) for d in range(2)]
+        wc = [sb.tile([P, N], U32, name=f"wc{d}", align_bytes=64) for d in range(2)]
         ws = [sb.tile([P, N], U8, name=f"ws{d}", align_bytes=64) for d in range(2)]
         gs = sb.tile([P, S], U8, name="gs", align_bytes=64)
-        wins = [[sb.tile([P, U], F32, name=f"win{d}{i}") for i in range(4 - d)] for d in range(2)]
-        win = [[wins[d][t % (4 - d)] for t in range(PACK)] for d in range(2)]
-        first = [sb.tile([P, U], F32, name=f"first{t}") for t in range(PACK)]
+        win = [[sb.tile([P, U], F32, name=f"win{d}{t}") for t in range(PACK)] for d in range(2)]
         total = sb.tile([P, PACK, U], F32, name="total")
         ob = sb.tile([P, U, PACK], BF16, name="ob", align_bytes=64)
         oc = sb.tile([P, U], I32, name="oc", align_bytes=64)
@@ -54,143 +46,134 @@ def tile_picked_spconv_none_po_kernel(
 
         w_rows = [w.rearrange("(p j) m -> p j m", j=PACK) for w in (w1, w2)]
 
+        def load_w(d, h):
+            nc.sync.dma_start(raw[d][h][:], w_rows[d][:, :, h * HALF : (h + 1) * HALF])
+
+        load_w(0, 0)
         nc.sync.dma_start(offs_t[:], offs)
         for q in range(4):
             rows = x_scales[0, 4 * q : 4 * q + 4, :].bitcast(I32)
             nc.sync.dma_start(xs[32 * q : 32 * q + 32, :].bitcast(I32), rows.partition_broadcast(8))
-        nc.sync.dma_start(raw[0][:], w_rows[0][:, :, 0:HALF])
+        load_w(0, 1)
         nc.sync.dma_start(xw[:], x_words[0].rearrange("p n r -> p (n r)").bitcast(I32))
         nc.sync.dma_start(to_t[0][:], to1)
-        nc.sync.dma_start(raw[1][:], w_rows[0][:, :, HALF:N])
-        for h in range(2):
-            nc.sync.dma_start(raw2[h][:], w_rows[1][:, :, h * HALF : (h + 1) * HALF])
+        load_w(1, 0)
+        load_w(1, 1)
         nc.sync.dma_start(to_t[1][:], to2)
 
         for d in range(2):
-            for w in wins[d]:
+            for w in win[d]:
                 (nc.gpsimd if d else nc.vector).memset(w[:], 0.0)
 
-        def deal_first(eng, h, rounded, a, b):
-            src = raw[h][:].rearrange("p j (l t) -> p l j t", t=PACK)[:, a:b]
-            dst = rounded[:].rearrange("p t l j -> p l j t")[:, a:b]
-            eng(dst, src)
-
         def pool_copy(dst, src):
-            order = "p m j t -> p m t j"
-            nc.gpsimd.tensor_scalar(dst.rearrange(order), src.rearrange(order), 1.0, 0.0, MULT, ADD)
+            nc.gpsimd.tensor_scalar(dst, src, 1.0, 0.0, MULT, ADD)
 
-        def deal_second(eng, h, a, b):
-            src = raw2[h][:].rearrange("p j (m t) -> p m j t", t=PACK)[:, a:b]
-            dst = wb2[:].rearrange("p t m j -> p m j t")[:, 64 * h + a : 64 * h + b]
+        def deal(eng, d, h, a, b):
+            src = raw[d][h][:].rearrange("p j (m t) -> p m t j", t=PACK)[:, a:b]
+            dst = wb[d][:].rearrange("p t m j -> p m t j")[:, 64 * h + a : 64 * h + b]
             eng(dst, src)
 
-        def quant_w(d, t0, t1, words, rounded):
+        def quant_w(d, t0, t1):
             nc.vector.quantize_mx(
-                out=words.bitcast(FP8X4),
+                out=wc[d][:, t0 * P : t1 * P].bitcast(FP8X4),
                 scales=ws[d][:, t0 * P : t1 * P],
-                in_=rounded,
+                in_=wb[d][:, t0:t1].rearrange("p t m j -> p (t m j)"),
             )
 
         def gather_words(a, b):
             nc.vector.tensor_copy(gw[:, a:b], xw[:].bitcast(U32).indirect(offs_t[:, a // 16 : b // 16]))
 
+        acc = {}
         ys = {}
-        tags = {(0, 3): "raw21"}
 
-        def multiply(d, t, a, b, acc):
+        def multiply(d, t):
+            acc[d, t] = ps.tile([P, V], F32, name=f"acc{d}{t}")
             nc.tensor.matmul_mx(
-                out=acc,
-                lhsT=codes[d][t].bitcast(FP8X4),
+                out=acc[d, t][:],
+                lhsT=wc[d][:, t * P : (t + 1) * P].bitcast(FP8X4),
                 lhsT_scale=ws[d][:, t * P : (t + 1) * P],
-                rhs=gw[:, d * V + a : d * V + b].bitcast(FP8X4),
-                rhs_scale=gs[:, d * V + a : d * V + b],
+                rhs=gw[:, d * V : (d + 1) * V].bitcast(FP8X4),
+                rhs_scale=gs[:, d * V : (d + 1) * V],
                 start=True,
                 stop=True,
             )
 
-        def empty(d, t, a, b, acc):
-            ys[d, t, a] = sb.tile([P, b - a], F32, name=f"y{d}{t}{a}", tag=tags.get((d, t), f"y{d}{t}{a}"))
-            nc.scalar.copy(ys[d, t, a][:], acc[:])
-            ys[d, t, a] = ys[d, t, a][:]
+        def empty(eng, d, t, a=0, b=V, tag=None):
+            y = sb.tile([P, b - a], F32, name=f"y{d}{t}{a}", tag=tag or f"y{d}{t}{a}", align_bytes=64)
+            eng(y[:], acc[d, t][:, a:b])
+            ys[d, t, a] = y
 
-        def product(d, t, a=0, b=V):
-            acc = ps.tile([P, b - a], F32, name=f"acc{d}{t}{a}", tag=f"acc{len(ys) % 8}")
-            multiply(d, t, a, b, acc[:])
-            empty(d, t, a, b, acc)
+        def scatter_v(d, t, a=0, b=V):
+            nc.vector.tensor_copy(win[d][t][:].indirect(to_t[d][:, a // 16 : b // 16]), ys[d, t, a][:])
 
-        def scatter(d, t, a=0, b=V):
-            nc.vector.tensor_copy(win[d][t][:].indirect(to_t[d][:, a // 16 : b // 16]), ys[d, t, a])
-
-        def move(blk):
-            h, pair = divmod(blk, 2)
-            for e in range(2):
-                nc.sync.dma_start(first[2 * pair + e][64 * h : 64 * h + 64, :], win[0][blk][64 * e : 64 * e + 64, :])
+        def scatter_s(d, t, a=0, b=V):
+            nc.scalar.activation(win[d][t][:].indirect(to_t[d][:, a // 16 : b // 16]), ys[d, t, a][:], COPY)
 
         out_rows = out_0.rearrange("(p t) u -> p t u", t=PACK)
 
-        def add(t, a, b):
-            eng = nc.gpsimd if t < 3 else nc.vector
-            eng.tensor_tensor(total[:, t, a:b], first[t][:, a:b], win[1][t][:, a:b], ADD)
+        def add(eng, t, a=0, b=U):
+            eng.tensor_tensor(total[:, t, a:b], win[0][t][:, a:b], win[1][t][:, a:b], ADD)
+
+        def store(t):
+            nc.sync.dma_start(out_rows[:, t, :], total[:, t, :])
 
         def weave(eng, t0, a, b):
             eng(ob[:, a:b, t0 : t0 + 2], total[:, t0 : t0 + 2, a:b].rearrange("p t u -> p u t"))
 
+        sc, vc = nc.scalar.copy, nc.vector.tensor_copy
+
         nc.vector.tensor_copy(gs[:], xs[:].indirect(offs_t[:]))
-        wb_a = sb.tile([P, PACK, 64, PACK], BF16, name="wb_a", align_bytes=64)
-        deal_first(nc.vector.tensor_copy, 0, wb_a, 0, 38)
-        deal_first(nc.scalar.copy, 0, wb_a, 38, 64)
-        quant_w(0, 0, 2, wc_a[:], wb_a[:].rearrange("p t m j -> p (t m j)"))
-        gw = sb.tile([P, S], U32, name="gw", tag="raw0", align_bytes=64)
-        gather_words(0, 128)
-        gather_words(128, V)
+        deal(sc, 0, 0, 0, 36)
+        deal(pool_copy, 0, 0, 36, 64)
+        deal(sc, 0, 1, 0, 20)
+        deal(pool_copy, 0, 1, 20, 36)
+        deal(vc, 0, 1, 36, 64)
+        quant_w(0, 0, 2)
+        gw = sb.tile([P, S], U32, name="gw", tag="raw01", align_bytes=64)
+        gather_words(0, V)
+        quant_w(0, 2, 4)
         gather_words(V, S)
-        product(0, 0, 0, 128)
-        product(0, 1, 0, 128)
-        held = ps.tile([P, 2, 128], F32, name="held", tag="acc2")
-        for blk in range(2):
-            multiply(0, blk, 128, V, held[:, blk])
-        wb_rest = sb.tile([P, PACK, 64, PACK], BF16, name="wb_rest", tag="mid0", align_bytes=64)
-        deal_first(pool_copy, 1, wb_rest, 0, 20)
-        deal_first(nc.scalar.copy, 1, wb_rest, 20, 64)
-        y_held = sb.tile([P, 2, 128], F32, name="y_held", tag="raw1", align_bytes=64)
-        nc.scalar.copy(y_held[:], held[:])
-        for blk in range(2):
-            ys[0, blk, 128] = y_held[:, blk]
-            scatter(0, blk, 0, 128)
-        quant_w(0, 2, 4, wc_rest[:], wb_rest[:].rearrange("p t m j -> p (t m j)"))
-        for blk in range(2):
-            scatter(0, blk, 128, V)
-            move(blk)
-        wb2 = sb.tile([P, PACK, P, PACK], BF16, name="wb2", tag="mid0", align_bytes=64)
-        deal_second(pool_copy, 0, 0, 40)
-        deal_second(nc.scalar.copy, 0, 40, 64)
-        product(0, 2)
-        deal_second(nc.scalar.copy, 1, 0, 64)
-        product(0, 3)
-        scatter(0, 2)
-        move(2)
-        quant_w(1, 0, 4, wc2[:], wb2[:].rearrange("p t m j -> p (t m j)"))
-        scatter(0, 3)
-        move(3)
+        for t in (1, 0, 2, 3):
+            multiply(0, t)
+        for h in range(2):
+            deal(pool_copy, 1, h, 0, 64)
+        empty(sc, 0, 1)
+        empty(sc, 0, 0)
+        empty(sc, 0, 2, 0, 128)
+        scatter_s(0, 1)
+        scatter_v(0, 0)
+        empty(sc, 0, 3)
+        scatter_s(0, 3)
+        scatter_v(0, 2, 0, 128)
+        empty(vc, 0, 2, 128, V, tag="raw11")
+        quant_w(1, 0, 2)
+        quant_w(1, 2, 4)
+        scatter_v(0, 2, 128, V)
         for t in range(PACK):
-            product(1, t)
-        for t in range(PACK - 1):
-            scatter(1, t)
-            add(t, 0, U)
-            nc.sync.dma_start(out_rows[:, t, :], total[:, t, :])
-            if t == 1:
-                weave(nc.scalar.copy, 0, 0, U)
-        scatter(1, 3)
+            multiply(1, t)
+        for t in range(PACK):
+            empty(sc, 1, t)
+        scatter_v(1, 0)
+        scatter_s(1, 1)
+        add(nc.gpsimd, 0)
+        store(0)
+        scatter_v(1, 2)
+        add(nc.gpsimd, 1)
+        store(1)
+        scatter_s(1, 3)
+        add(nc.vector, 2)
+        store(2)
+        weave(vc, 0, 0, U)
         words = out_1[0].rearrange("p u r -> p (u r)").bitcast(I32)
         cut = 192
         mid = (cut + U) // 2
-        add(3, 0, cut)
-        weave(nc.scalar.copy, 2, 0, cut)
-        add(3, cut, mid)
-        add(3, mid, U)
-        nc.sync.dma_start(out_rows[:, 3, :], total[:, 3, :])
-        weave(nc.vector.tensor_copy, 2, cut, mid)
-        weave(nc.vector.tensor_copy, 2, mid, U)
+        add(nc.vector, 3, 0, cut)
+        weave(sc, 2, 0, cut)
+        add(nc.vector, 3, cut, mid)
+        add(nc.vector, 3, mid, U)
+        store(3)
+        weave(vc, 2, cut, mid)
+        weave(vc, 2, mid, U)
         for h in range(2):
             c = slice(h * 256, (h + 1) * 256)
             nc.vector.quantize_mx(

@@ -28,12 +28,21 @@ def tile_picked_spconv_none_po_kernel(
     with ExitStack() as ctx:
         sb = ctx.enter_context(tc.tile_pool(name="sb", bufs=1))
         ps = ctx.enter_context(tc.psum_pool(name="ps", bufs=1))
+        shared = ctx.enter_context(tc.tile_pool(name="shared", bufs=1))
 
         offs_t = sb.tile([P, S // 16], U16, name="offs_t")
         to_t = [sb.tile([P, V // 16], U16, name=f"to_t{d}") for d in range(2)]
         xw = sb.tile([P, T], I32, name="xw", align_bytes=64)
         xs = sb.tile([P, T], U8, name="xs", align_bytes=64)
-        raw = [[sb.tile([P, PACK, HALF], F32, name=f"raw{d}{h}", tag=f"raw{d}{h}", align_bytes=64) for h in range(2)] for d in range(2)]
+        raw = [
+            [
+                shared.tile([P, PACK, HALF], F32, name="raw11", offset=0)
+                if d and h
+                else sb.tile([P, PACK, HALF], F32, name=f"raw{d}{h}", tag=f"raw{d}{h}", align_bytes=64)
+                for h in range(2)
+            ]
+            for d in range(2)
+        ]
         wb = [sb.tile([P, PACK, P, PACK], BF16, name=f"wb{d}", align_bytes=64) for d in range(2)]
         wc = [sb.tile([P, N], U32, name=f"wc{d}", align_bytes=64) for d in range(2)]
         ws = [sb.tile([P, N], U8, name=f"ws{d}", align_bytes=64) for d in range(2)]
@@ -83,31 +92,43 @@ def tile_picked_spconv_none_po_kernel(
         def gather_words(a, b):
             nc.vector.tensor_copy(gw[:, a:b], xw[:].bitcast(U32).indirect(offs_t[:, a // 16 : b // 16]))
 
-        acc = {}
         ys = {}
 
-        def multiply(d, t):
-            acc[d, t] = ps.tile([P, V], F32, name=f"acc{d}{t}")
-            nc.tensor.matmul_mx(
-                out=acc[d, t][:],
-                lhsT=wc[d][:, t * P : (t + 1) * P].bitcast(FP8X4),
-                lhsT_scale=ws[d][:, t * P : (t + 1) * P],
-                rhs=gw[:, d * V : (d + 1) * V].bitcast(FP8X4),
-                rhs_scale=gs[:, d * V : (d + 1) * V],
-                start=True,
-                stop=True,
-            )
+        def products(name, parts):
+            bank = ps.tile([P, sum(b - a for d, t, a, b in parts)], F32, name=name)
+            at = 0
+            for d, t, a, b in parts:
+                nc.tensor.matmul_mx(
+                    out=bank[:, at : at + b - a],
+                    lhsT=wc[d][:, t * P : (t + 1) * P].bitcast(FP8X4),
+                    lhsT_scale=ws[d][:, t * P : (t + 1) * P],
+                    rhs=gw[:, d * V + a : d * V + b].bitcast(FP8X4),
+                    rhs_scale=gs[:, d * V + a : d * V + b],
+                    start=True,
+                    stop=True,
+                )
+                at += b - a
+            return name, bank, parts
 
-        def empty(eng, d, t, a=0, b=V, tag=None):
-            y = sb.tile([P, b - a], F32, name=f"y{d}{t}{a}", tag=tag or f"y{d}{t}{a}", align_bytes=64)
-            eng(y[:], acc[d, t][:, a:b])
-            ys[d, t, a] = y
+        def empty(eng, made, tag=None, pieces=None, start=0, offset=None):
+            name, bank, parts = made
+            pieces = pieces or parts
+            width = sum(b - a for d, t, a, b in pieces)
+            if offset is None:
+                y = sb.tile([P, width], F32, name=f"y_{name}{start}", tag=tag or f"y_{name}{start}", align_bytes=64)
+            else:
+                y = shared.tile([P, width], F32, name=f"y_{name}{start}", offset=offset)
+            eng(y[:], bank[:, start : start + width])
+            at = 0
+            for d, t, a, b in pieces:
+                ys[d, t, a] = y[:, at : at + b - a]
+                at += b - a
 
         def scatter_v(d, t, a=0, b=V):
-            nc.vector.tensor_copy(win[d][t][:].indirect(to_t[d][:, a // 16 : b // 16]), ys[d, t, a][:])
+            nc.vector.tensor_copy(win[d][t][:].indirect(to_t[d][:, a // 16 : b // 16]), ys[d, t, a])
 
         def scatter_s(d, t, a=0, b=V):
-            nc.scalar.activation(win[d][t][:].indirect(to_t[d][:, a // 16 : b // 16]), ys[d, t, a][:], COPY)
+            nc.scalar.activation(win[d][t][:].indirect(to_t[d][:, a // 16 : b // 16]), ys[d, t, a], COPY)
 
         out_rows = out_0.rearrange("(p t) u -> p t u", t=PACK)
 
@@ -130,50 +151,54 @@ def tile_picked_spconv_none_po_kernel(
         deal(vc, 0, 1, 36, 64)
         quant_w(0, 0, 2)
         gw = sb.tile([P, S], U32, name="gw", tag="raw01", align_bytes=64)
-        gather_words(0, V)
+        gather_words(0, 128)
+        gather_words(128, V)
         quant_w(0, 2, 4)
         gather_words(V, S)
-        for t in (1, 0, 2, 3):
-            multiply(0, t)
+        lead_s = products("lead_s", [(0, 1, 0, 128)])
+        lead_v = products("lead_v", [(0, 0, 0, V)])
+        second = products("second", [(0, 1, 128, V), (0, 3, 0, V)])
+        third = products("third", [(0, 2, 0, V)])
         for h in range(2):
             deal(pool_copy, 1, h, 0, 64)
-        empty(sc, 0, 1)
-        empty(sc, 0, 0)
-        empty(sc, 0, 2, 0, 128)
-        scatter_s(0, 1)
+        empty(sc, lead_s, tag="y_s")
+        empty(vc, lead_v)
+        scatter_s(0, 1, 0, 128)
         scatter_v(0, 0)
-        empty(sc, 0, 3)
-        scatter_s(0, 3)
-        scatter_v(0, 2, 0, 128)
-        empty(vc, 0, 2, 128, V, tag="raw11")
+        empty(sc, second, tag="y_s", pieces=[(0, 1, 128, V), (0, 3, 0, 192)])
+        scatter_s(0, 1, 128, V)
+        scatter_s(0, 3, 0, 192)
         quant_w(1, 0, 2)
+        empty(vc, third, offset=0)
+        empty(vc, second, pieces=[(0, 3, 192, V)], start=320, offset=4 * V)
         quant_w(1, 2, 4)
-        scatter_v(0, 2, 128, V)
-        for t in range(PACK):
-            multiply(1, t)
-        for t in range(PACK):
-            empty(sc, 1, t)
-        scatter_v(1, 0)
+        scatter_v(0, 2)
+        scatter_v(0, 3, 192, V)
+        late = [products(f"late{t}", [(1, t, 0, V)]) for t in (1, 0, 2, 3)]
+        empty(sc, late[0])
+        empty(sc, late[1])
         scatter_s(1, 1)
-        add(nc.gpsimd, 0)
-        store(0)
+        scatter_v(1, 0)
+        empty(sc, late[2])
+        empty(sc, late[3], tag="y_late10")
         scatter_v(1, 2)
+        scatter_s(1, 3)
         add(nc.gpsimd, 1)
         store(1)
-        scatter_s(1, 3)
+        add(nc.gpsimd, 0, 0, 256)
+        add(nc.gpsimd, 0, 256, U)
+        store(0)
         add(nc.vector, 2)
         store(2)
-        weave(vc, 0, 0, U)
         words = out_1[0].rearrange("p u r -> p (u r)").bitcast(I32)
-        cut = 192
-        mid = (cut + U) // 2
-        add(nc.vector, 3, 0, cut)
-        weave(sc, 2, 0, cut)
-        add(nc.vector, 3, cut, mid)
-        add(nc.vector, 3, mid, U)
+        weave(sc, 0, 0, 256)
+        weave(sc, 0, 256, U)
+        add(nc.vector, 3, 256, U)
+        add(nc.vector, 3, 0, 256)
         store(3)
-        weave(vc, 2, cut, mid)
-        weave(vc, 2, mid, U)
+        weave(vc, 2, 256, 352)
+        weave(vc, 2, 0, 256)
+        weave(sc, 2, 352, U)
         for h in range(2):
             c = slice(h * 256, (h + 1) * 256)
             nc.vector.quantize_mx(

@@ -138,8 +138,8 @@ def tile_picked_spconv_none_po_kernel(
         def store(t):
             nc.sync.dma_start(out_rows[:, t, :], total[:, t, :])
 
-        def weave(eng, t0, a, b):
-            eng(ob[:, a:b, t0 : t0 + 2], total[:, t0 : t0 + 2, a:b].rearrange("p t u -> p u t"))
+        def weave(eng, a, b):
+            eng(ob[:, a:b, :], total[:, :, a:b].rearrange("p t u -> p u t"))
 
         sc, vc = nc.scalar.copy, nc.vector.tensor_copy
 
@@ -185,20 +185,17 @@ def tile_picked_spconv_none_po_kernel(
         scatter_s(1, 3)
         add(nc.gpsimd, 1)
         store(1)
-        add(nc.gpsimd, 0, 0, 256)
-        add(nc.gpsimd, 0, 256, U)
+        add(nc.gpsimd, 0)
         store(0)
-        add(nc.vector, 2)
-        store(2)
         words = out_1[0].rearrange("p u r -> p (u r)").bitcast(I32)
-        weave(sc, 0, 0, 256)
-        weave(sc, 0, 256, U)
-        add(nc.vector, 3, 256, U)
-        add(nc.vector, 3, 0, 256)
+        for a in (256, 0):
+            add(nc.vector, 2, a, a + 256)
+            add(nc.vector, 3, a, a + 256)
+        store(2)
         store(3)
-        weave(vc, 2, 256, 352)
-        weave(vc, 2, 0, 256)
-        weave(sc, 2, 352, U)
+        weave(sc, 304, U)
+        weave(vc, 256, 304)
+        weave(vc, 0, 256)
         for h in range(2):
             c = slice(h * 256, (h + 1) * 256)
             nc.vector.quantize_mx(

@@ -159,29 +159,31 @@ def tile_picked_spconv_none_po_kernel(
         lead_v = products("lead_v", [(0, 0, 0, V)])
         second = products("second", [(0, 1, 128, V), (0, 3, 0, V)])
         third = products("third", [(0, 2, 0, V)])
-        for h in range(2):
-            deal(pool_copy, 1, h, 0, 64)
+        deal(pool_copy, 1, 0, 0, 32)
+        deal(pool_copy, 1, 1, 0, 64)
         empty(sc, lead_s, tag="y_s")
         empty(vc, lead_v)
         scatter_s(0, 1, 0, 128)
         scatter_v(0, 0)
-        empty(sc, second, tag="y_s", pieces=[(0, 1, 128, V), (0, 3, 0, 192)])
+        deal(sc, 1, 0, 32, 64)
+        empty(sc, second, tag="y_s", pieces=[(0, 1, 128, V), (0, 3, 0, 128)])
         scatter_s(0, 1, 128, V)
-        scatter_s(0, 3, 0, 192)
+        scatter_s(0, 3, 0, 128)
         quant_w(1, 0, 2)
         empty(vc, third, offset=0)
-        empty(vc, second, pieces=[(0, 3, 192, V)], start=320, offset=4 * V)
+        empty(vc, second, pieces=[(0, 3, 128, V)], start=256, offset=4 * V)
         quant_w(1, 2, 4)
         scatter_v(0, 2)
-        scatter_v(0, 3, 192, V)
+        scatter_v(0, 3, 128, V)
         late = [products(f"late{t}", [(1, t, 0, V)]) for t in (1, 0, 2, 3)]
         empty(sc, late[0])
         empty(sc, late[1])
         scatter_s(1, 1)
         scatter_v(1, 0)
-        empty(sc, late[2])
+        empty(sc, late[2], pieces=[(1, 2, 0, 64), (1, 2, 64, V)])
         empty(sc, late[3], tag="y_late10")
-        scatter_v(1, 2)
+        scatter_s(1, 2, 0, 64)
+        scatter_v(1, 2, 64, V)
         scatter_s(1, 3)
         add(nc.gpsimd, 1)
         store(1)

@@ -58,11 +58,16 @@ def tile_picked_spconv_none_po_kernel(
         def load_w(d, h):
             nc.sync.dma_start(raw[d][h][:], w_rows[d][:, :, h * HALF : (h + 1) * HALF])
 
-        load_w(0, 0)
-        nc.sync.dma_start(offs_t[:], offs)
-        for q in range(4):
+        def load_scales(q):
             rows = x_scales[0, 4 * q : 4 * q + 4, :].bitcast(I32)
-            nc.sync.dma_start(xs[32 * q : 32 * q + 32, :].bitcast(I32), rows.partition_broadcast(8))
+            nc.sync.dma_start(xs[32 * q : 32 * q + 4, :].bitcast(I32), rows)
+
+        nc.gpsimd.memset(xs[:].bitcast(I32), 0)
+        nc.sync.dma_start(offs_t[:], offs)
+        load_scales(0)
+        load_w(0, 0)
+        for q in range(1, 4):
+            load_scales(q)
         load_w(0, 1)
         nc.sync.dma_start(xw[:], x_words[0].rearrange("p n r -> p (n r)").bitcast(I32))
         nc.sync.dma_start(to_t[0][:], to1)

@@ -43,7 +43,7 @@ def tile_picked_spconv_none_po_kernel(
             ]
             for d in range(2)
         ]
-        wb = [sb.tile([P, PACK, P, PACK], BF16, name=f"wb{d}", align_bytes=64) for d in range(2)]
+        wb = [sb.tile([P, PACK, P, PACK], BF16, name="wb0", tag="wb", align_bytes=64)]
         wc = [sb.tile([P, N], U32, name=f"wc{d}", align_bytes=64) for d in range(2)]
         ws = [sb.tile([P, N], U8, name=f"ws{d}", align_bytes=64) for d in range(2)]
         gs = sb.tile([P, S], U8, name="gs", align_bytes=64)
@@ -151,8 +151,8 @@ def tile_picked_spconv_none_po_kernel(
         nc.vector.tensor_copy(gs[:], xs[:].indirect(offs_t[:]))
         deal(sc, 0, 0, 0, 36)
         deal(pool_copy, 0, 0, 36, 64)
-        deal(sc, 0, 1, 0, 20)
-        deal(pool_copy, 0, 1, 20, 36)
+        deal(sc, 0, 1, 0, 24)
+        deal(pool_copy, 0, 1, 24, 36)
         deal(vc, 0, 1, 36, 64)
         quant_w(0, 0, 2)
         gw = sb.tile([P, S], U32, name="gw", tag="raw01", align_bytes=64)
@@ -163,46 +163,48 @@ def tile_picked_spconv_none_po_kernel(
         lead_s = products("lead_s", [(0, 1, 0, 128)])
         lead_v = products("lead_v", [(0, 0, 0, V)])
         second = products("second", [(0, 1, 128, V), (0, 3, 0, V)])
-        third = products("third", [(0, 2, 0, V)])
-        deal(pool_copy, 1, 0, 0, 32)
+        third = products("third", [(0, 2, 0, 128)])
+        wb.append(sb.tile([P, PACK, P, PACK], BF16, name="wb1", tag="wb", align_bytes=64))
+        deal(pool_copy, 1, 0, 0, 48)
         deal(pool_copy, 1, 1, 0, 64)
         empty(sc, lead_s, tag="y_s")
         empty(vc, lead_v)
         scatter_s(0, 1, 0, 128)
         scatter_v(0, 0)
-        deal(sc, 1, 0, 32, 64)
-        empty(sc, second, tag="y_s", pieces=[(0, 1, 128, V), (0, 3, 0, 128)])
+        deal(sc, 1, 0, 48, 64)
+        empty(sc, second, tag="y_s", pieces=[(0, 1, 128, V), (0, 3, 0, 160)])
         scatter_s(0, 1, 128, V)
-        scatter_s(0, 3, 0, 128)
+        scatter_s(0, 3, 0, 160)
         quant_w(1, 0, 2)
         empty(vc, third, offset=0)
-        empty(vc, second, pieces=[(0, 3, 128, V)], start=256, offset=4 * V)
+        empty(vc, second, pieces=[(0, 3, 160, V)], start=288, offset=4 * V)
         quant_w(1, 2, 4)
-        scatter_v(0, 2)
-        scatter_v(0, 3, 128, V)
-        late = [products(f"late{t}", [(1, t, 0, V)]) for t in (1, 0, 2, 3)]
+        scatter_v(0, 2, 0, 128)
+        scatter_v(0, 3, 160, V)
+        late = [products(f"late{t}", [(1, t, 0, V)] + [(0, t, 128, V)] * (t == 2)) for t in (1, 0, 2, 3)]
         empty(sc, late[0])
-        empty(sc, late[1])
+        empty(vc, late[1])
+        empty(vc, late[2])
         scatter_s(1, 1)
         scatter_v(1, 0)
-        empty(sc, late[2], pieces=[(1, 2, 0, 64), (1, 2, 64, V)])
         empty(sc, late[3], tag="y_late10")
-        scatter_s(1, 2, 0, 64)
-        scatter_v(1, 2, 64, V)
+        scatter_s(0, 2, 128, V)
+        scatter_v(1, 2)
         scatter_s(1, 3)
         add(nc.gpsimd, 1)
         store(1)
         add(nc.gpsimd, 0)
         store(0)
         words = out_1[0].rearrange("p u r -> p (u r)").bitcast(I32)
-        for a in (256, 0):
-            add(nc.vector, 2, a, a + 256)
-            add(nc.vector, 3, a, a + 256)
+        add(nc.vector, 2)
         store(2)
+        for a, b in ((384, U), (0, 256), (256, 384)):
+            add(nc.vector, 3, a, b)
         store(3)
-        weave(sc, 304, U)
-        weave(vc, 256, 304)
+        weave(sc, 384, U)
         weave(vc, 0, 256)
+        weave(sc, 304, 384)
+        weave(vc, 256, 304)
         for h in range(2):
             c = slice(h * 256, (h + 1) * 256)
             nc.vector.quantize_mx(

@@ -18,7 +18,20 @@ COPY = mybir.ActivationFunctionType.Copy
 
 P = 128
 PACK = 4
-HALF = N // 2
+QUADS = 4
+STRIPE = 16
+HALF_COLS = N // 2
+HALF_L = P // 2
+HALF_V = V // 2
+HALF_U = U // 2
+
+W1A_SCALAR = 36
+W1B_SCALAR, W1B_GPSIMD = 24, 36
+W2A_GPSIMD = 36
+WEAVE_FIRST, WEAVE_SCALAR = 384, 304
+
+RAW_BYTES = PACK * HALF_COLS * 4
+PIECE_BYTES = HALF_V * 4
 
 
 def tile_picked_spconv_none_po_kernel(
@@ -30,187 +43,202 @@ def tile_picked_spconv_none_po_kernel(
         ps = ctx.enter_context(tc.psum_pool(name="ps", bufs=1))
         shared = ctx.enter_context(tc.tile_pool(name="shared", bufs=1))
 
-        offs_t = sb.tile([P, S // 16], U16, name="offs_t")
-        to_t = [sb.tile([P, V // 16], U16, name=f"to_t{d}") for d in range(2)]
-        xw = sb.tile([P, T], I32, name="xw", align_bytes=64)
-        xs = sb.tile([P, T], U8, name="xs", align_bytes=64)
+        offs_t = sb.tile([P, S // STRIPE], U16, name="offs_t")
+        to_t = [sb.tile([P, V // STRIPE], U16, name=f"to_t{d}") for d in range(2)]
+        table_words = sb.tile([P, T], I32, name="table_words", align_bytes=64)
+        table_scales = sb.tile([P, T], U8, name="table_scales", align_bytes=64)
         raw = [
             [
-                shared.tile([P, PACK, HALF], F32, name="raw11", offset=0)
+                shared.tile([P, PACK, HALF_COLS], F32, name="raw11", offset=0, align_bytes=64)
                 if d and h
-                else sb.tile([P, PACK, HALF], F32, name=f"raw{d}{h}", tag=f"raw{d}{h}", align_bytes=64)
+                else sb.tile([P, PACK, HALF_COLS], F32, name=f"raw{d}{h}", tag=f"raw{d}{h}", align_bytes=64)
                 for h in range(2)
             ]
             for d in range(2)
         ]
-        wb = [sb.tile([P, PACK, P, PACK], BF16, name="wb0", tag="wb", align_bytes=64)]
-        wc = [sb.tile([P, N], U32, name=f"wc{d}", align_bytes=64) for d in range(2)]
-        ws = [sb.tile([P, N], U8, name=f"ws{d}", align_bytes=64) for d in range(2)]
-        gs = sb.tile([P, S], U8, name="gs", align_bytes=64)
-        win = [[sb.tile([P, U], F32, name=f"win{d}{t}") for t in range(PACK)] for d in range(2)]
+        rounded = [sb.tile([P, PACK, P, PACK], BF16, name="rounded0", tag="rounded", align_bytes=64)]
+        w_codes = [sb.tile([P, N], U32, name=f"w_codes{d}", align_bytes=64) for d in range(2)]
+        w_scales = [sb.tile([P, N], U8, name=f"w_scales{d}", align_bytes=64) for d in range(2)]
+        picked_scales = sb.tile([P, S], U8, name="picked_scales", align_bytes=64)
+        window = [[sb.tile([P, U], F32, name=f"window{d}{t}") for t in range(PACK)] for d in range(2)]
         total = sb.tile([P, PACK, U], F32, name="total")
-        ob = sb.tile([P, U, PACK], BF16, name="ob", align_bytes=64)
-        oc = sb.tile([P, U], I32, name="oc", align_bytes=64)
-        osc = sb.tile([P, U], U8, name="osc", align_bytes=64)
+        woven = sb.tile([P, U, PACK], BF16, name="woven", align_bytes=64)
+        out_codes = sb.tile([P, U], I32, name="out_codes", align_bytes=64)
+        out_scales = sb.tile([P, U], U8, name="out_scales", align_bytes=64)
 
         w_rows = [w.rearrange("(p j) m -> p j m", j=PACK) for w in (w1, w2)]
+        out_rows = out_0.rearrange("(p t) u -> p t u", t=PACK)
+        out_words = out_1[0].rearrange("p u r -> p (u r)").bitcast(I32)
 
         def load_w(d, h):
-            nc.sync.dma_start(raw[d][h][:], w_rows[d][:, :, h * HALF : (h + 1) * HALF])
+            nc.sync.dma_start(raw[d][h][:], w_rows[d][:, :, h * HALF_COLS : (h + 1) * HALF_COLS])
 
-        def load_scales(q):
-            rows = x_scales[0, 4 * q : 4 * q + 4, :].bitcast(I32)
-            nc.sync.dma_start(xs[32 * q : 32 * q + 4, :].bitcast(I32), rows)
-
-        nc.gpsimd.memset(xs[:].bitcast(I32), 0)
-        nc.sync.dma_start(offs_t[:], offs)
-        load_scales(0)
+        nc.gpsimd.memset(table_scales[:].bitcast(I32), 0)
         load_w(0, 0)
-        for q in range(1, 4):
-            load_scales(q)
+        nc.sync.dma_start(offs_t[:], offs)
+        for q in range(QUADS):
+            rows = x_scales[0, 4 * q : 4 * q + 4, :].bitcast(I32)
+            nc.sync.dma_start(table_scales[32 * q : 32 * q + 4, :].bitcast(I32), rows)
         load_w(0, 1)
-        nc.sync.dma_start(xw[:], x_words[0].rearrange("p n r -> p (n r)").bitcast(I32))
+        nc.sync.dma_start(table_words[:], x_words[0].rearrange("p n r -> p (n r)").bitcast(I32))
         nc.sync.dma_start(to_t[0][:], to1)
         load_w(1, 0)
         load_w(1, 1)
         nc.sync.dma_start(to_t[1][:], to2)
 
         for d in range(2):
-            for w in win[d]:
-                (nc.gpsimd if d else nc.vector).memset(w[:], 0.0)
+            for tile in window[d]:
+                (nc.gpsimd if d else nc.vector).memset(tile[:], 0.0)
 
-        def pool_copy(dst, src):
+        scalar_copy, vector_copy = nc.scalar.copy, nc.vector.tensor_copy
+
+        def gpsimd_copy(dst, src):
             nc.gpsimd.tensor_scalar(dst, src, 1.0, 0.0, MULT, ADD)
 
-        def deal(eng, d, h, a, b):
-            src = raw[d][h][:].rearrange("p j (m t) -> p m t j", t=PACK)[:, a:b]
-            dst = wb[d][:].rearrange("p t m j -> p m t j")[:, 64 * h + a : 64 * h + b]
-            eng(dst, src)
+        def deal(copy, d, h, a, b):
+            src = raw[d][h][:].rearrange("p j (l t) -> p l j t", t=PACK)[:, a:b]
+            dst = rounded[d][:].rearrange("p t l j -> p l j t")[:, HALF_L * h + a : HALF_L * h + b]
+            copy(dst, src)
 
-        def quant_w(d, t0, t1):
+        def quantise_w(d, t0, t1):
             nc.vector.quantize_mx(
-                out=wc[d][:, t0 * P : t1 * P].bitcast(FP8X4),
-                scales=ws[d][:, t0 * P : t1 * P],
-                in_=wb[d][:, t0:t1].rearrange("p t m j -> p (t m j)"),
+                out=w_codes[d][:, t0 * P : t1 * P].bitcast(FP8X4),
+                scales=w_scales[d][:, t0 * P : t1 * P],
+                in_=rounded[d][:, t0:t1].rearrange("p t l j -> p (t l j)"),
             )
 
         def gather_words(a, b):
-            nc.vector.tensor_copy(gw[:, a:b], xw[:].bitcast(U32).indirect(offs_t[:, a // 16 : b // 16]))
+            source = table_words[:].bitcast(U32).indirect(offs_t[:, a // STRIPE : b // STRIPE])
+            nc.vector.tensor_copy(picked_words[:, a:b], source)
 
-        ys = {}
+        in_sbuf = {}
 
-        def products(name, parts):
-            bank = ps.tile([P, sum(b - a for d, t, a, b in parts)], F32, name=name)
+        def multiply(name, pieces):
+            bank = ps.tile([P, sum(b - a for d, t, a, b in pieces)], F32, name=name)
             at = 0
-            for d, t, a, b in parts:
+            for d, t, a, b in pieces:
                 nc.tensor.matmul_mx(
                     out=bank[:, at : at + b - a],
-                    lhsT=wc[d][:, t * P : (t + 1) * P].bitcast(FP8X4),
-                    lhsT_scale=ws[d][:, t * P : (t + 1) * P],
-                    rhs=gw[:, d * V + a : d * V + b].bitcast(FP8X4),
-                    rhs_scale=gs[:, d * V + a : d * V + b],
+                    lhsT=w_codes[d][:, t * P : (t + 1) * P].bitcast(FP8X4),
+                    lhsT_scale=w_scales[d][:, t * P : (t + 1) * P],
+                    rhs=picked_words[:, d * V + a : d * V + b].bitcast(FP8X4),
+                    rhs_scale=picked_scales[:, d * V + a : d * V + b],
                     start=True,
                     stop=True,
                 )
                 at += b - a
-            return name, bank, parts
+            return bank
 
-        def empty(eng, made, tag=None, pieces=None, start=0, offset=None):
-            name, bank, parts = made
-            pieces = pieces or parts
+        def to_sbuf(copy, bank, start, pieces, offset=None):
             width = sum(b - a for d, t, a, b in pieces)
+            name = "piece%d%d_%d" % pieces[0][:3]
             if offset is None:
-                y = sb.tile([P, width], F32, name=f"y_{name}{start}", tag=tag or f"y_{name}{start}", align_bytes=64)
+                tile = sb.tile([P, width], F32, name=name, align_bytes=64)
             else:
-                y = shared.tile([P, width], F32, name=f"y_{name}{start}", offset=offset)
-            eng(y[:], bank[:, start : start + width])
+                tile = shared.tile([P, width], F32, name=name, offset=offset, align_bytes=64)
+            copy(tile[:], bank[:, start : start + width])
             at = 0
-            for d, t, a, b in pieces:
-                ys[d, t, a] = y[:, at : at + b - a]
-                at += b - a
+            for piece in pieces:
+                in_sbuf[piece] = tile[:, at : at + piece[3] - piece[2]]
+                at += piece[3] - piece[2]
 
-        def scatter_v(d, t, a=0, b=V):
-            nc.vector.tensor_copy(win[d][t][:].indirect(to_t[d][:, a // 16 : b // 16]), ys[d, t, a])
+        def target(piece):
+            d, t, a, b = piece
+            return window[d][t][:].indirect(to_t[d][:, a // STRIPE : b // STRIPE])
 
-        def scatter_s(d, t, a=0, b=V):
-            nc.scalar.activation(win[d][t][:].indirect(to_t[d][:, a // 16 : b // 16]), ys[d, t, a], COPY)
+        def vector_scatter(piece):
+            nc.vector.tensor_copy(target(piece), in_sbuf[piece])
 
-        out_rows = out_0.rearrange("(p t) u -> p t u", t=PACK)
+        def scalar_scatter(piece):
+            nc.scalar.activation(target(piece), in_sbuf[piece], COPY)
 
-        def add(eng, t, a=0, b=U):
-            eng.tensor_tensor(total[:, t, a:b], win[0][t][:, a:b], win[1][t][:, a:b], ADD)
+        def add(engine, t, a=0, b=U):
+            engine.tensor_tensor(total[:, t, a:b], window[0][t][:, a:b], window[1][t][:, a:b], ADD)
 
         def store(t):
             nc.sync.dma_start(out_rows[:, t, :], total[:, t, :])
 
-        def weave(eng, a, b):
-            eng(ob[:, a:b, :], total[:, :, a:b].rearrange("p t u -> p u t"))
-
-        sc, vc = nc.scalar.copy, nc.vector.tensor_copy
-
-        nc.vector.tensor_copy(gs[:], xs[:].indirect(offs_t[:]))
-        deal(sc, 0, 0, 0, 36)
-        deal(pool_copy, 0, 0, 36, 64)
-        deal(sc, 0, 1, 0, 24)
-        deal(pool_copy, 0, 1, 24, 36)
-        deal(vc, 0, 1, 36, 64)
-        quant_w(0, 0, 2)
-        gw = sb.tile([P, S], U32, name="gw", tag="raw01", align_bytes=64)
-        gather_words(0, 128)
-        gather_words(128, V)
-        quant_w(0, 2, 4)
-        gather_words(V, S)
-        lead_s = products("lead_s", [(0, 1, 0, 128)])
-        lead_v = products("lead_v", [(0, 0, 0, V)])
-        second = products("second", [(0, 1, 128, V), (0, 3, 0, V)])
-        third = products("third", [(0, 2, 0, 128)])
-        wb.append(sb.tile([P, PACK, P, PACK], BF16, name="wb1", tag="wb", align_bytes=64))
-        deal(pool_copy, 1, 0, 0, 48)
-        deal(pool_copy, 1, 1, 0, 64)
-        empty(sc, lead_s, tag="y_s")
-        empty(vc, lead_v)
-        scatter_s(0, 1, 0, 128)
-        scatter_v(0, 0)
-        deal(sc, 1, 0, 48, 64)
-        empty(sc, second, tag="y_s", pieces=[(0, 1, 128, V), (0, 3, 0, 160)])
-        scatter_s(0, 1, 128, V)
-        scatter_s(0, 3, 0, 160)
-        quant_w(1, 0, 2)
-        empty(vc, third, offset=0)
-        empty(vc, second, pieces=[(0, 3, 160, V)], start=288, offset=4 * V)
-        quant_w(1, 2, 4)
-        scatter_v(0, 2, 0, 128)
-        scatter_v(0, 3, 160, V)
-        late = [products(f"late{t}", [(1, t, 0, V)] + [(0, t, 128, V)] * (t == 2)) for t in (1, 0, 2, 3)]
-        empty(sc, late[0])
-        empty(vc, late[1])
-        empty(vc, late[2])
-        scatter_s(1, 1)
-        scatter_v(1, 0)
-        empty(sc, late[3], tag="y_late10")
-        scatter_s(0, 2, 128, V)
-        scatter_v(1, 2)
-        scatter_s(1, 3)
-        add(nc.gpsimd, 1)
-        store(1)
-        add(nc.gpsimd, 0)
-        store(0)
-        words = out_1[0].rearrange("p u r -> p (u r)").bitcast(I32)
-        add(nc.vector, 2)
-        store(2)
-        for a, b in ((384, U), (0, 256), (256, 384)):
-            add(nc.vector, 3, a, b)
-        store(3)
-        weave(sc, 384, U)
-        weave(vc, 0, 256)
-        weave(sc, 304, 384)
-        weave(vc, 256, 304)
-        for h in range(2):
-            c = slice(h * 256, (h + 1) * 256)
-            nc.vector.quantize_mx(
-                out=oc[:, c].bitcast(FP8X4), scales=osc[:, c], in_=ob[:, c, :].rearrange("p u t -> p (u t)")
+        def weave(copy, a, b):
+            copy(
+                woven[:, a:b, :].rearrange("p (c i) t -> p c t i", i=4),
+                total[:, :, a:b].rearrange("p t (c i) -> p c t i", i=4),
             )
-            nc.sync.dma_start(words[:, c], oc[:, c])
-        for q in range(4):
-            eng = nc.scalar if q % 2 else nc.sync
-            eng.dma_start(out_2[0, 4 * q : 4 * q + 4, :].bitcast(I32), osc[32 * q : 32 * q + 4, :].bitcast(I32))
+
+        low = [(0, t, 0, HALF_V) for t in range(PACK)]
+        high = [(0, t, HALF_V, V) for t in range(PACK)]
+        second_tap = [(1, t, 0, V) for t in range(PACK)]
+
+        nc.vector.tensor_copy(picked_scales[:], table_scales[:].indirect(offs_t[:]))
+        deal(scalar_copy, 0, 0, 0, W1A_SCALAR)
+        deal(gpsimd_copy, 0, 0, W1A_SCALAR, HALF_L)
+        deal(scalar_copy, 0, 1, 0, W1B_SCALAR)
+        deal(gpsimd_copy, 0, 1, W1B_SCALAR, W1B_GPSIMD)
+        deal(vector_copy, 0, 1, W1B_GPSIMD, HALF_L)
+        quantise_w(0, 0, 2)
+        picked_words = sb.tile([P, S], U32, name="picked_words", tag="raw01", align_bytes=64)
+        gather_words(0, HALF_V)
+        quantise_w(0, 2, PACK)
+        gather_words(HALF_V, V)
+        gather_words(V, S)
+
+        bank_s0 = multiply("bank_s0", [low[1]])
+        bank_v0 = multiply("bank_v0", [low[0]])
+        bank_v1 = multiply("bank_v1", [low[2], high[0]])
+        bank_s1 = multiply("bank_s1", [high[1], (0, 3, 0, V)])
+        rounded.append(sb.tile([P, PACK, P, PACK], BF16, name="rounded1", tag="rounded", align_bytes=64))
+        deal(gpsimd_copy, 1, 0, 0, W2A_GPSIMD)
+        deal(gpsimd_copy, 1, 1, 0, HALF_L)
+        to_sbuf(scalar_copy, bank_s0, 0, [low[1]], offset=RAW_BYTES + PIECE_BYTES // 2)
+        to_sbuf(scalar_copy, bank_v0, 0, [low[0]])
+        to_sbuf(vector_copy, bank_v1, 0, [low[2]])
+        scalar_scatter(low[1])
+        vector_scatter(low[0])
+        vector_scatter(low[2])
+        deal(scalar_copy, 1, 0, W2A_GPSIMD, HALF_L)
+        to_sbuf(scalar_copy, bank_s1, 0, [high[1]], offset=RAW_BYTES)
+        to_sbuf(scalar_copy, bank_s1, HALF_V, [low[3]], offset=RAW_BYTES + PIECE_BYTES)
+        scalar_scatter(high[1])
+        scalar_scatter(low[3])
+
+        quantise_w(1, 0, 2)
+        to_sbuf(vector_copy, bank_v1, HALF_V, [high[0]], offset=0)
+        to_sbuf(vector_copy, bank_s1, V, [high[3]], offset=2 * PIECE_BYTES)
+        quantise_w(1, 2, PACK)
+        vector_scatter(high[0])
+        vector_scatter(high[3])
+
+        early_planes = (1, 0, 3)
+        banks = [multiply(f"bank_tap1_{t}", [second_tap[t]]) for t in early_planes]
+        last_bank = multiply("bank_last", [second_tap[2], high[2]])
+        for t, bank in zip(early_planes, banks):
+            to_sbuf(scalar_copy, bank, 0, [second_tap[t]])
+        to_sbuf(vector_copy, last_bank, 0, [second_tap[2], high[2]])
+        scalar_scatter(second_tap[1])
+        vector_scatter(second_tap[0])
+        scalar_scatter(second_tap[3])
+        vector_scatter(second_tap[2])
+        scalar_scatter(high[2])
+
+        for engine, t in ((nc.gpsimd, 1), (nc.gpsimd, 0), (nc.vector, 3)):
+            add(engine, t)
+            store(t)
+        for a, b in ((WEAVE_FIRST, U), (0, HALF_U), (HALF_U, WEAVE_FIRST)):
+            add(nc.vector, 2, a, b)
+        store(2)
+        weave(scalar_copy, WEAVE_FIRST, U)
+        weave(vector_copy, 0, HALF_U)
+        weave(scalar_copy, WEAVE_SCALAR, WEAVE_FIRST)
+        weave(vector_copy, HALF_U, WEAVE_SCALAR)
+        for h in range(2):
+            cols = slice(h * HALF_U, (h + 1) * HALF_U)
+            nc.vector.quantize_mx(
+                out=out_codes[:, cols].bitcast(FP8X4),
+                scales=out_scales[:, cols],
+                in_=woven[:, cols, :].rearrange("p u t -> p (u t)"),
+            )
+            nc.sync.dma_start(out_words[:, cols], out_codes[:, cols])
+        for q in range(QUADS):
+            queue = nc.scalar if q % 2 else nc.sync
+            queue.dma_start(
+                out_2[0, 4 * q : 4 * q + 4, :].bitcast(I32), out_scales[32 * q : 32 * q + 4, :].bitcast(I32)
+            )

@@ -87,8 +87,8 @@ def tile_picked_spconv_none_po_kernel(
         nc.sync.dma_start(to_t[1][:], to2)
 
         for d in range(2):
-            for tile in window[d]:
-                (nc.gpsimd if d else nc.vector).memset(tile[:], 0.0)
+            for t in range(PACK):
+                (nc.gpsimd if d and t >= 2 else nc.vector).memset(window[d][t][:], 0.0)
 
         scalar_copy, vector_copy = nc.scalar.copy, nc.vector.tensor_copy
 
@@ -183,14 +183,14 @@ def tile_picked_spconv_none_po_kernel(
 
         bank_s0 = multiply("bank_s0", [low[1]])
         bank_v0 = multiply("bank_v0", [low[0]])
-        bank_v1 = multiply("bank_v1", [low[2], high[0]])
-        bank_s1 = multiply("bank_s1", [high[1], (0, 3, 0, V)])
+        bank_v1 = multiply("bank_v1", [low[2]])
+        bank_s1 = multiply("bank_s1", [high[1], (0, 3, 0, V), high[0]])
         rounded.append(sb.tile([P, PACK, P, PACK], BF16, name="rounded1", tag="rounded", align_bytes=64))
         deal(gpsimd_copy, 1, 0, 0, W2A_GPSIMD)
         deal(gpsimd_copy, 1, 1, 0, HALF_L)
         to_sbuf(scalar_copy, bank_s0, 0, [low[1]], offset=RAW_BYTES + PIECE_BYTES // 2)
         to_sbuf(scalar_copy, bank_v0, 0, [low[0]])
-        to_sbuf(vector_copy, bank_v1, 0, [low[2]])
+        to_sbuf(scalar_copy, bank_v1, 0, [low[2]])
         scalar_scatter(low[1])
         vector_scatter(low[0])
         vector_scatter(low[2])
@@ -201,8 +201,7 @@ def tile_picked_spconv_none_po_kernel(
         scalar_scatter(low[3])
 
         quantise_w(1, 0, 2)
-        to_sbuf(vector_copy, bank_v1, HALF_V, [high[0]], offset=0)
-        to_sbuf(vector_copy, bank_s1, V, [high[3]], offset=2 * PIECE_BYTES)
+        to_sbuf(vector_copy, bank_s1, V, [high[3], high[0]], offset=0)
         quantise_w(1, 2, PACK)
         vector_scatter(high[0])
         vector_scatter(high[3])

@@ -27,11 +27,12 @@ HALF_U = U // 2
 
 W1A_SCALAR = 36
 W1B_SCALAR, W1B_GPSIMD = 24, 36
-W2A_GPSIMD = 36
+W2B_GPSIMD = 40
 WEAVE_FIRST, WEAVE_SCALAR = 384, 304
 
 RAW_BYTES = PACK * HALF_COLS * 4
 PIECE_BYTES = HALF_V * 4
+FIRST_PIECE = RAW_BYTES + 2 * PIECE_BYTES
 
 
 def tile_picked_spconv_none_po_kernel(
@@ -109,7 +110,7 @@ def tile_picked_spconv_none_po_kernel(
 
         def gather_words(a, b):
             source = table_words[:].bitcast(U32).indirect(offs_t[:, a // STRIPE : b // STRIPE])
-            nc.vector.tensor_copy(picked_words[:, a:b], source)
+            nc.vector.tensor_copy(picked_words[a // V][:, a % V : a % V + b - a], source)
 
         in_sbuf = {}
 
@@ -121,7 +122,7 @@ def tile_picked_spconv_none_po_kernel(
                     out=bank[:, at : at + b - a],
                     lhsT=w_codes[d][:, t * P : (t + 1) * P].bitcast(FP8X4),
                     lhsT_scale=w_scales[d][:, t * P : (t + 1) * P],
-                    rhs=picked_words[:, d * V + a : d * V + b].bitcast(FP8X4),
+                    rhs=picked_words[d][:, a:b].bitcast(FP8X4),
                     rhs_scale=picked_scales[:, d * V + a : d * V + b],
                     start=True,
                     stop=True,
@@ -175,26 +176,27 @@ def tile_picked_spconv_none_po_kernel(
         deal(gpsimd_copy, 0, 1, W1B_SCALAR, W1B_GPSIMD)
         deal(vector_copy, 0, 1, W1B_GPSIMD, HALF_L)
         quantise_w(0, 0, 2)
-        picked_words = sb.tile([P, S], U32, name="picked_words", tag="raw01", align_bytes=64)
+        picked_words = [sb.tile([P, V], U32, name="picked_words0", tag="raw01", align_bytes=64)]
         gather_words(0, HALF_V)
         quantise_w(0, 2, PACK)
         gather_words(HALF_V, V)
-        gather_words(V, S)
 
-        bank_s0 = multiply("bank_s0", [low[1]])
         bank_v0 = multiply("bank_v0", [low[0]])
+        bank_s0 = multiply("bank_s0", [low[1]])
         bank_v1 = multiply("bank_v1", [low[2]])
         bank_s1 = multiply("bank_s1", [high[1], (0, 3, 0, V), high[0]])
         rounded.append(sb.tile([P, PACK, P, PACK], BF16, name="rounded1", tag="rounded", align_bytes=64))
-        deal(gpsimd_copy, 1, 0, 0, W2A_GPSIMD)
-        deal(gpsimd_copy, 1, 1, 0, HALF_L)
+        deal(gpsimd_copy, 1, 0, 0, HALF_L)
+        deal(gpsimd_copy, 1, 1, 0, W2B_GPSIMD)
+        to_sbuf(scalar_copy, bank_v0, 0, [low[0]], offset=FIRST_PIECE)
         to_sbuf(scalar_copy, bank_s0, 0, [low[1]], offset=RAW_BYTES + PIECE_BYTES // 2)
-        to_sbuf(scalar_copy, bank_v0, 0, [low[0]])
         to_sbuf(scalar_copy, bank_v1, 0, [low[2]])
         scalar_scatter(low[1])
         vector_scatter(low[0])
         vector_scatter(low[2])
-        deal(scalar_copy, 1, 0, W2A_GPSIMD, HALF_L)
+        picked_words.append(shared.tile([P, V], U32, name="picked_words1", offset=FIRST_PIECE, align_bytes=64))
+        gather_words(V, S)
+        deal(scalar_copy, 1, 1, W2B_GPSIMD, HALF_L)
         to_sbuf(scalar_copy, bank_s1, 0, [high[1]], offset=RAW_BYTES)
         to_sbuf(scalar_copy, bank_s1, HALF_V, [low[3]], offset=RAW_BYTES + PIECE_BYTES)
         scalar_scatter(high[1])

from contextlib import ExitStack

import concourse.mybir as mybir

K, T, S, V, N, U = 512, 1024, 512, 256, 512, 512
FLOPS = 2 * 2 * K * N * V

F32 = mybir.dt.float32
BF16 = mybir.dt.bfloat16
I32 = mybir.dt.int32
U32 = mybir.dt.uint32
U16 = mybir.dt.uint16
U8 = mybir.dt.uint8
FP8X4 = mybir.dt.float8_e4m3fn_x4
ADD = mybir.AluOpType.add
MULT = mybir.AluOpType.mult
COPY = mybir.ActivationFunctionType.Copy

P = 128
PACK = 4
QUADS = 4
STRIPE = 16
HALF_COLS = N // 2
HALF_L = P // 2
HALF_V = V // 2
HALF_U = U // 2

W1A_SCALAR = 36
W1B_SCALAR, W1B_GPSIMD = 24, 36
W2B_GPSIMD = 40
WEAVE_FIRST, WEAVE_SCALAR = 384, 304

RAW_BYTES = PACK * HALF_COLS * 4
PIECE_BYTES = HALF_V * 4
FIRST_PIECE = RAW_BYTES + 2 * PIECE_BYTES


def tile_picked_spconv_none_po_kernel(
    tc, x_words, x_scales, w1, w2, offs, to1, to2, out_0, out_1, out_2
):
    nc = tc.nc
    with ExitStack() as ctx:
        sb = ctx.enter_context(tc.tile_pool(name="sb", bufs=1))
        ps = ctx.enter_context(tc.psum_pool(name="ps", bufs=1))
        shared = ctx.enter_context(tc.tile_pool(name="shared", bufs=1))

        offs_t = sb.tile([P, S // STRIPE], U16, name="offs_t")
        to_t = [sb.tile([P, V // STRIPE], U16, name=f"to_t{d}") for d in range(2)]
        table_words = sb.tile([P, T], I32, name="table_words", align_bytes=64)
        table_scales = sb.tile([P, T], U8, name="table_scales", align_bytes=64)
        raw = [
            [
                shared.tile([P, PACK, HALF_COLS], F32, name="raw11", offset=0, align_bytes=64)
                if d and h
                else sb.tile([P, PACK, HALF_COLS], F32, name=f"raw{d}{h}", tag=f"raw{d}{h}", align_bytes=64)
                for h in range(2)
            ]
            for d in range(2)
        ]
        rounded = [sb.tile([P, PACK, P, PACK], BF16, name="rounded0", tag="rounded", align_bytes=64)]
        w_codes = [sb.tile([P, N], U32, name=f"w_codes{d}", align_bytes=64) for d in range(2)]
        w_scales = [sb.tile([P, N], U8, name=f"w_scales{d}", align_bytes=64) for d in range(2)]
        picked_scales = sb.tile([P, S], U8, name="picked_scales", align_bytes=64)
        window = [[sb.tile([P, U], F32, name=f"window{d}{t}") for t in range(PACK)] for d in range(2)]
        total = sb.tile([P, PACK, U], F32, name="total")
        woven = sb.tile([P, U, PACK], BF16, name="woven", align_bytes=64)
        out_codes = sb.tile([P, U], I32, name="out_codes", align_bytes=64)
        out_scales = sb.tile([P, U], U8, name="out_scales", align_bytes=64)

        w_rows = [w.rearrange("(p j) m -> p j m", j=PACK) for w in (w1, w2)]
        out_rows = out_0.rearrange("(p t) u -> p t u", t=PACK)
        out_words = out_1[0].rearrange("p u r -> p (u r)").bitcast(I32)

        def load_w(d, h):
            nc.sync.dma_start(raw[d][h][:], w_rows[d][:, :, h * HALF_COLS : (h + 1) * HALF_COLS])

        nc.gpsimd.memset(table_scales[:].bitcast(I32), 0)
        load_w(0, 0)
        nc.sync.dma_start(offs_t[:], offs)
        for q in range(QUADS):
            rows = x_scales[0, 4 * q : 4 * q + 4, :].bitcast(I32)
            nc.sync.dma_start(table_scales[32 * q : 32 * q + 4, :].bitcast(I32), rows)
        load_w(0, 1)
        nc.sync.dma_start(table_words[:], x_words[0].rearrange("p n r -> p (n r)").bitcast(I32))
        nc.sync.dma_start(to_t[0][:], to1)
        load_w(1, 0)
        load_w(1, 1)
        nc.sync.dma_start(to_t[1][:], to2)

        for d in range(2):
            for t in range(PACK):
                (nc.gpsimd if d and t >= 2 else nc.vector).memset(window[d][t][:], 0.0)

        scalar_copy, vector_copy = nc.scalar.copy, nc.vector.tensor_copy

        def gpsimd_copy(dst, src):
            nc.gpsimd.tensor_scalar(dst, src, 1.0, 0.0, MULT, ADD)

        def deal(copy, d, h, a, b):
            src = raw[d][h][:].rearrange("p j (l t) -> p l j t", t=PACK)[:, a:b]
            dst = rounded[d][:].rearrange("p t l j -> p l j t")[:, HALF_L * h + a : HALF_L * h + b]
            copy(dst, src)

        def quantise_w(d, t0, t1):
            nc.vector.quantize_mx(
                out=w_codes[d][:, t0 * P : t1 * P].bitcast(FP8X4),
                scales=w_scales[d][:, t0 * P : t1 * P],
                in_=rounded[d][:, t0:t1].rearrange("p t l j -> p (t l j)"),
            )

        def gather_words(a, b):
            source = table_words[:].bitcast(U32).indirect(offs_t[:, a // STRIPE : b // STRIPE])
            nc.vector.tensor_copy(picked_words[a // V][:, a % V : a % V + b - a], source)

        in_sbuf = {}

        def multiply(name, pieces):
            bank = ps.tile([P, sum(b - a for d, t, a, b in pieces)], F32, name=name)
            at = 0
            for d, t, a, b in pieces:
                nc.tensor.matmul_mx(
                    out=bank[:, at : at + b - a],
                    lhsT=w_codes[d][:, t * P : (t + 1) * P].bitcast(FP8X4),
                    lhsT_scale=w_scales[d][:, t * P : (t + 1) * P],
                    rhs=picked_words[d][:, a:b].bitcast(FP8X4),
                    rhs_scale=picked_scales[:, d * V + a : d * V + b],
                    start=True,
                    stop=True,
                )
                at += b - a
            return bank

        def to_sbuf(copy, bank, start, pieces, offset=None):
            width = sum(b - a for d, t, a, b in pieces)
            name = "piece%d%d_%d" % pieces[0][:3]
            if offset is None:
                tile = sb.tile([P, width], F32, name=name, align_bytes=64)
            else:
                tile = shared.tile([P, width], F32, name=name, offset=offset, align_bytes=64)
            copy(tile[:], bank[:, start : start + width])
            at = 0
            for piece in pieces:
                in_sbuf[piece] = tile[:, at : at + piece[3] - piece[2]]
                at += piece[3] - piece[2]

        def target(piece):
            d, t, a, b = piece
            return window[d][t][:].indirect(to_t[d][:, a // STRIPE : b // STRIPE])

        def vector_scatter(piece):
            nc.vector.tensor_copy(target(piece), in_sbuf[piece])

        def scalar_scatter(piece):
            nc.scalar.activation(target(piece), in_sbuf[piece], COPY)

        def add(engine, t, a=0, b=U):
            engine.tensor_tensor(total[:, t, a:b], window[0][t][:, a:b], window[1][t][:, a:b], ADD)

        def store(t):
            nc.sync.dma_start(out_rows[:, t, :], total[:, t, :])

        def weave(copy, a, b):
            copy(
                woven[:, a:b, :].rearrange("p (c i) t -> p c t i", i=4),
                total[:, :, a:b].rearrange("p t (c i) -> p c t i", i=4),
            )

        low = [(0, t, 0, HALF_V) for t in range(PACK)]
        high = [(0, t, HALF_V, V) for t in range(PACK)]
        second_tap = [(1, t, 0, V) for t in range(PACK)]

        nc.vector.tensor_copy(picked_scales[:], table_scales[:].indirect(offs_t[:]))
        deal(scalar_copy, 0, 0, 0, W1A_SCALAR)
        deal(gpsimd_copy, 0, 0, W1A_SCALAR, HALF_L)
        deal(scalar_copy, 0, 1, 0, W1B_SCALAR)
        deal(gpsimd_copy, 0, 1, W1B_SCALAR, W1B_GPSIMD)
        deal(vector_copy, 0, 1, W1B_GPSIMD, HALF_L)
        quantise_w(0, 0, 2)
        picked_words = [sb.tile([P, V], U32, name="picked_words0", tag="raw01", align_bytes=64)]
        gather_words(0, HALF_V)
        quantise_w(0, 2, PACK)
        gather_words(HALF_V, V)

        bank_v0 = multiply("bank_v0", [low[0]])
        bank_s0 = multiply("bank_s0", [low[1]])
        bank_v1 = multiply("bank_v1", [low[2]])
        bank_s1 = multiply("bank_s1", [high[1], (0, 3, 0, V), high[0]])
        rounded.append(sb.tile([P, PACK, P, PACK], BF16, name="rounded1", tag="rounded", align_bytes=64))
        deal(gpsimd_copy, 1, 0, 0, HALF_L)
        deal(gpsimd_copy, 1, 1, 0, W2B_GPSIMD)
        to_sbuf(scalar_copy, bank_v0, 0, [low[0]], offset=FIRST_PIECE)
        to_sbuf(scalar_copy, bank_s0, 0, [low[1]], offset=RAW_BYTES + PIECE_BYTES // 2)
        to_sbuf(scalar_copy, bank_v1, 0, [low[2]])
        scalar_scatter(low[1])
        vector_scatter(low[0])
        vector_scatter(low[2])
        picked_words.append(shared.tile([P, V], U32, name="picked_words1", offset=FIRST_PIECE, align_bytes=64))
        gather_words(V, S)
        deal(scalar_copy, 1, 1, W2B_GPSIMD, HALF_L)
        to_sbuf(scalar_copy, bank_s1, 0, [high[1]], offset=RAW_BYTES)
        to_sbuf(scalar_copy, bank_s1, HALF_V, [low[3]], offset=RAW_BYTES + PIECE_BYTES)
        scalar_scatter(high[1])
        scalar_scatter(low[3])

        quantise_w(1, 0, 2)
        to_sbuf(vector_copy, bank_s1, V, [high[3], high[0]], offset=0)
        quantise_w(1, 2, PACK)
        vector_scatter(high[0])
        vector_scatter(high[3])

        early_planes = (1, 0, 3)
        banks = [multiply(f"bank_tap1_{t}", [second_tap[t]]) for t in early_planes]
        last_bank = multiply("bank_last", [second_tap[2], high[2]])
        for t, bank in zip(early_planes, banks):
            to_sbuf(scalar_copy, bank, 0, [second_tap[t]])
        to_sbuf(vector_copy, last_bank, 0, [second_tap[2], high[2]])
        scalar_scatter(second_tap[1])
        vector_scatter(second_tap[0])
        scalar_scatter(second_tap[3])
        vector_scatter(second_tap[2])
        scalar_scatter(high[2])

        for engine, t in ((nc.gpsimd, 1), (nc.gpsimd, 0), (nc.vector, 3)):
            add(engine, t)
            store(t)
        for a, b in ((WEAVE_FIRST, U), (0, HALF_U), (HALF_U, WEAVE_FIRST)):
            add(nc.vector, 2, a, b)
        store(2)
        weave(scalar_copy, WEAVE_FIRST, U)
        weave(vector_copy, 0, HALF_U)
        weave(scalar_copy, WEAVE_SCALAR, WEAVE_FIRST)
        weave(vector_copy, HALF_U, WEAVE_SCALAR)
        for h in range(2):
            cols = slice(h * HALF_U, (h + 1) * HALF_U)
            nc.vector.quantize_mx(
                out=out_codes[:, cols].bitcast(FP8X4),
                scales=out_scales[:, cols],
                in_=woven[:, cols, :].rearrange("p u t -> p (u t)"),
            )
            nc.sync.dma_start(out_words[:, cols], out_codes[:, cols])
        for q in range(QUADS):
            queue = nc.scalar if q % 2 else nc.sync
            queue.dma_start(
                out_2[0, 4 * q : 4 * q + 4, :].bitcast(I32), out_scales[32 * q : 32 * q + 4, :].bitcast(I32)
            )
